import numpy as np, ml_dtypes
CORES = [24,25,26,27,28,29,30,31]
N = 8
BF = ml_dtypes.bfloat16
def gentries(a):
    return np.ascontiguousarray(a.reshape(8, 16, -1).transpose(0, 2, 1)).reshape(8, -1)
def gtable(e):
    e = np.asarray(e); return np.ascontiguousarray(e.reshape(8, -1, 16).transpose(0, 2, 1)).reshape(128, -1).astype(np.int32)
W, K, RO, S, TH, AG = 2048, 384, 2, 4, 70, 9
L0 = 16 - RO
B = K // N
def hubbed(rng, hub, n, share):
    return np.where(rng.random((N, 8, n)) < share, np.take_along_axis(hub, rng.integers(0, 32, (N, 8, n)), 2), rng.integers(0, W, (N, 8, n)))
def parts(rng):
    x = np.where(rng.random((N, 8, 1, W)) < 0.875, rng.integers(0, 16, (N, 8, 16, W)), rng.integers(4, 12, (N, 8, 16, W)))
    hub = rng.integers(0, W, (N, 8, 32)); a = hubbed(rng, hub, L0 * W, 0.1).reshape(N, 8, L0, W)
    a = np.where(rng.random(a.shape) < rng.choice(np.array([0.05, 0.2, 0.45]), (N, 8, 1, 1)), -1, a)
    return x, a, hubbed(rng, hub, W, 0.25), rng.integers(0, W, (N, 8, K))
def pack(x, a, s, p):
    a = np.concatenate([a, np.full((N, 8, RO, W), -1)], axis=2)
    return {"x0": np.ascontiguousarray(x.reshape(N, 128, W)).astype(np.float32).astype(BF), "lk": np.ascontiguousarray(a.reshape(N, 128, W)).astype(np.int32),
            "nx": np.ascontiguousarray(s).astype(np.int32), "w0": np.stack([gtable(e) for e in p])}
def setup_inputs(rng):
    return pack(*parts(rng))
def setup_inputs_ties(rng):
    x, a, s, p = parts(rng); h = W // 2
    x[..., :h] = rng.integers(0, 16, (N, 8, 16, h))
    t = TH - 1 + rng.integers(0, 3, (N, 8, 1, h)); o = np.argsort(rng.random((N, 8, 16, h)), axis=2)
    x[..., h:2 * h] = x[..., :h] + np.where(x[..., :h] < 8, 1, -1) * ((t >> 4) + (o < (t & 15)))
    i = np.arange(L0)[None, None, :, None]; at = rng.integers(0, L0, (N, 8, 1, h)); bare = rng.random((N, 8, 1, h)) < 0.5
    a[..., :h] = np.where(i == at, h + np.arange(h), np.where((i > at) | bare, -1, a[..., :h]))
    return pack(x, a, s, rng.integers(0, h, (N, 8, K)))
def setup_inputs_votes(rng):
    x, a, s, p = parts(rng); h = K // 2
    for q in range(N):
        for g in range(8):
            if q < N - 1 and g % 4 == 3: continue
            c = rng.permutation(W)[:K * (S + 1)].reshape(K, S + 1); a[q, g] = -1
            s[q, g, c[:, :S]] = c[:, 1:]
            if q == N - 1:
                y = rng.integers(5, 8, (16, K, S)); e = np.where(np.arange(K) < h, 15, rng.integers(8, 11, (16, K)))
                s[q, g, c[:h, S]] = c[h + rng.permutation(h), 2]
                p[q, g] = c[:, 0]
            elif g % 2 == 1:
                n = K - 1 if g == 1 else int(rng.integers(h, K))
                y = rng.integers(0, 8, (16, K, S)); y[rng.permutation(16)[AG - 1:], n] += 8
                e = rng.integers(0, 16, (16, K)); e[:, 0] = 8
                s[q, g, c[:, S - 1]] = c[0, S]
                p[q, g] = c[:, 0]
            else:
                y = rng.integers(2, 14, (16, K, S)); y[:, h:] = np.where(rng.random((1, K - h, 1)) < 0.5, 2, 13)
                z = y[:, :, 0]
                for k in range(1, S): z = (z + y[:, :, k]) >> 1
                o = np.argsort(rng.random((16, K)), axis=0); n = AG - 1 + rng.integers(0, 3, (1, K))
                e = z + np.where(o < n, rng.integers(1, 3, (16, K)), -rng.integers(0, 2, (16, K)))
                s[q, g, c[h:, S - 1]] = np.where(rng.random(K - h) < 0.75, c[:K - h, S], c[h:, S])
                p[q, g] = c[rng.permutation(K), 0]
            x[q, g][:, c[:, :S].reshape(-1)] = y.reshape(16, K * S); x[q, g][:, c[:, S]] = e
    return pack(x, a, s, p)
def setup_inputs_alike(rng):
    x, a, s, p = parts(rng); few = np.array([0, W - 1, W // 2, 5])
    a[:, ::2] = np.where(a[:, ::2] < 0, -1, rng.choice(few, (N, 4, L0, W)))
    a[:, 1] = np.where(a[:, 1] < 0, -1, np.arange(W)); s[:, 1] = np.arange(W)
    s[:, 0] = W - 1; s[:, 4] = 0; s[:, 2] = rng.choice(few, (N, W))
    p[:, 3] = p[:, 3, :1]; p[:, 5] = rng.choice(few, (N, K)); p[:, 6] = np.where(rng.random((N, K)) < 0.5, 0, W - 1)
    return pack(x, a, s, p)
def setup_inputs_full(rng):
    x, a, s, p = parts(rng)
    x[:, ::2] = rng.integers(6, 10, (N, 4, 16, W)); x[:, 1::2] = 15 * rng.integers(0, 2, (N, 4, 16, W))
    a = np.where(a < 0, rng.integers(0, W, a.shape), a)
    return pack(x, a, s, p)
def setup_inputs_spread(rng):
    x, a, s, p = parts(rng)
    x = np.minimum((np.exp2(1 + 3 * rng.random((N, 8, 1, W))) * rng.random((N, 8, 16, W))).astype(np.int64), 15)
    a = np.where(a < 0, -1, (W * rng.random(a.shape) ** 3).astype(np.int64)); s = (W * rng.random(s.shape) ** 2).astype(np.int64)
    return pack(x, np.minimum(a, W - 1), np.minimum(s, W - 1), p)
def check_inputs(d):
    bad = []
    x = d["x0"].astype(np.float32)
    if not np.all((x >= 0) & (x <= 15) & (x == np.floor(x))): bad.append("x0 whole numbers from 0 to 15")
    for k, lo in (("lk", -1), ("nx", 0), ("w0", 0)):
        if np.min(d[k]) < lo or np.max(d[k]) > W - 1: bad.append("range of " + k)
    if np.any(d["lk"].reshape(-1, 8, 16, W)[:, :, L0:] != -1): bad.append("upper links of lk empty")
    return bad
def reference(x0, lk, nx, w0):
    M = W + RO * K
    X = np.zeros((N, 8, 16, M), np.int64); X[..., :W] = x0.astype(np.float32).astype(np.int64).reshape(N, 8, 16, W)
    ad = np.full((N, 8, 16, M), -1, np.int64); ad[..., :W] = lk.reshape(N, 8, 16, W)
    sc = np.zeros((N, 8, M), np.int64); sc[..., :W] = nx
    v = np.stack([gentries(e) for e in w0]).astype(np.int64)
    i = np.arange(16)[:, None]
    for t in range(RO):
        n = W + t * K; Z = np.zeros((N, 8, 16, K), np.int64)
        for r in range(N):
            for g in range(8):
                x, a, s, p = X[r, g], ad[r, g], sc[r, g], v[r, g]
                z = x[:, p]; l = np.full(K, 16)
                for k in range(S):
                    c = a[:, p]
                    dist = np.add.reduce(np.abs(x[:, np.maximum(c, 0)] - z[:, None, :]), axis=0)
                    b = np.max(np.where((c >= 0) & (dist < TH) & (i < l), i, -1), axis=0)
                    p = np.where(b >= 0, c[np.maximum(b, 0), np.arange(K)], s[p]); l = np.where(b >= 0, b, l)
                    y = x[:, p]; yes = np.add.reduce((y > z).astype(np.int64), axis=0) >= AG
                    z = (z + y) >> 1
                Z[r, g] = z; v[r, g] = p
                ends = np.zeros(M, bool); ends[p] = True
                no = np.zeros(M, bool); no[p[~yes]] = True
                x[::2] = np.where(ends & ~no, 15 - x[::2], x[::2])
                u, first = np.unique(p, return_index=True)
                a[L0 + t, u] = n + first; s[n:n + K] = s[p]
        for r in range(N):
            for q in range(N):
                X[q, :, :, n + r * B:n + (r + 1) * B] = np.roll(Z[r, :, :, q * B:(q + 1) * B], (q - r) % N, axis=0)
    return {"yx": X.reshape(N, 128, M).astype(np.float32).astype(BF), "yv": v.astype(np.float32)}

@@ -1,0 +1,510 @@
+from concourse.bass import DstId, RemoteDMATransfer
+from concourse.mybir import AluOpType, ActivationFunctionType
+
+ALU = AluOpType
+ACT = ActivationFunctionType
+H = 8 + 2816
+NA = 2816 + 384
+EPS = 2.0 ** -9
+
+SCRATCH = {}
+
+
+def _decl(dtype, where="sbuf", **shapes):
+    for n, sh in shapes.items():
+        SCRATCH[n] = (where, [128] + sh, dtype)
+
+
+_decl("bfloat16", X2=[2 * H], XO=[8 + NA], W3=[768], ZD=[144], BK=[128], ID=[128], NI=[128], PN=[128], DW=[128], TU=[128],
+      ZR=[128], SWB=[512], R1=[384], DIAG=[24, 16], TRI=[24, 16], E=[576, 16], DG=[24, 16], DX=[384], FX=[384], FL=[384],
+      XV=[384], XW=[384], ZN0=[384], ZN1=[384], RZ0=[384], RZ1=[384])
+_decl("float32", AT=[NA], IDT=[2816], C=[32], Q=[144], QX=[24, 16], QX2=[128], QG=[128], T1=[128], T2=[128], SWF=[512],
+      NEWL=[384], DWL=[24], VLF=[24], WT=[24], VF=[384], DM=[384], SC2=[384], S1=[24], S2=[24], S3=[24], S4=[24],
+      GA=[384], GA3=[24, 16])
+_decl("int32", ATI=[2048], W0I=[24], PI=[8], QW=[768])
+_decl("uint16", VL0=[24], VX0=[24], VXN=[24], VB=[48, 16], AOFF=[24], XOFF=[24])
+for _s in "AB":
+    _decl("bfloat16", **{"CD" + _s: [3072], "AB" + _s: [3072], "XG" + _s: [384], "Z" + _s: [384], "ZF" + _s: [12, 16],
+                         "VAL" + _s: [192], "F" + _s: [192], "GT" + _s: [192]})
+    _decl("float32", **{"LT" + _s: [192], "KT" + _s: [192], "SC" + _s: [192]})
+    _decl("int32", **{"VI" + _s: [12], "VJ" + _s: [12]})
+    _decl("uint16", **{"CL" + _s: [192]})
+    _decl("float32", "psum", **{"pD" + _s: [512], "pK" + _s: [32, 16], "pZ" + _s: [32, 16], "pS" + _s: [32, 16]})
+SEMAPHORES = ["sv", "ss", "sp", "sg", "dw", "dl", "dx", "dy", "dd", "do", "dv", "dgA", "dgB", "arr0", "arr1", "lsem"]
+
+
+def make_emitter(g, T):
+    eng = {"V": g.vector, "S": g.scalar, "P": g.tensor, "G": g, "Y": g.sync}
+    sem = {"V": "sv", "S": "ss", "P": "sp", "G": "sg"}
+    cnt = {}
+    know = {e: {} for e in eng}
+    lastw, readers, snaps = {}, {}, {}
+
+    def wait_for(e, r, w):
+        need = []
+        for k in r:
+            if k in lastw:
+                need.append((lastw[k], False))
+            if k[0] == "p":
+                need.extend((x, True) for x in readers.get(k, ()))
+        for k in w:
+            if k in lastw:
+                need.append((lastw[k], True))
+            need.extend((x, True) for x in readers.get(k, ()))
+        mx = {}
+        for (s, c), anti in need:
+            if s == e and (anti or e == "P"):
+                continue
+            if s not in eng:
+                c = cnt[s]
+            if know[e].get(s, 0) < c:
+                mx[s] = max(mx.get(s, 0), c)
+        for s in list(mx):
+            if any(s2 != s and mx[s2] and snaps.get((s2, mx[s2]), {}).get(s, 0) >= mx[s] for s2 in mx):
+                know[e][s] = max(know[e].get(s, 0), mx[s])
+                mx[s] = 0
+        for s, c in mx.items():
+            if c:
+                eng[e].wait_ge(T.sem[sem.get(s, s)], c)
+                for s2, c2 in snaps.get((s, c), {}).items():
+                    know[e][s2] = max(know[e].get(s2, 0), c2)
+                know[e][s] = max(know[e].get(s, 0), c)
+
+    def note(tok, e, r, w):
+        sn = dict(know[e])
+        if tok[0] in eng:
+            sn[tok[0]] = tok[1]
+        else:
+            for s2, c2 in snaps.get((tok[0], tok[1] - 16), {}).items():
+                sn[s2] = max(sn.get(s2, 0), c2)
+        snaps[tok] = sn
+        for k in r:
+            readers.setdefault(k, []).append(tok)
+        for k in w:
+            lastw[k] = tok
+            readers[k] = []
+
+    def op(e, fn, r=(), w=()):
+        wait_for(e, r, w)
+        cnt[e] = cnt.get(e, 0) + 1
+        fn(eng[e]).then_inc(T.sem[sem[e]], 1)
+        note((e, cnt[e]), e, r, w)
+
+    def dma(e, out, in_, s, r=(), w=()):
+        wait_for(e, r, w)
+        cnt[s] = cnt.get(s, 0) + 16
+        eng[e].dma_start(out=out, in_=in_).then_inc(T.sem[s], 16)
+        note((s, cnt[s]), e, r, w)
+
+    def arrive(s, c, key):
+        cnt[s] = c
+        lastw[key] = (s, c)
+
+    def finish():
+        for s, c in sorted(cnt.items()):
+            if know["G"].get(s, 0) < c:
+                g.wait_ge(T.sem[sem.get(s, s)], c)
+    return op, dma, arrive, finish, wait_for
+
+
+def rank_program(g, core, T, topo):
+    rank = T.rank_of(core)
+    if rank is None:
+        return
+    op, dma, arrive, finish, wait_for = make_emitter(g, T)
+
+    def V(fn, r=(), w=()):
+        op("V", fn, r, w)
+
+    def ts(out, in0, s1, s2, op0, op1, r, w):
+        if op1 is None:
+            V(lambda v: v.tensor_scalar(out, in0, s1, None, op0), r, w)
+        else:
+            V(lambda v: v.tensor_scalar(out, in0, s1, s2, op0, op1), r, w)
+
+    def tt(out, in0, in1, o, r, w):
+        V(lambda v: v.tensor_tensor(out, in0, in1, o), r, w)
+
+    def cp(out, in_, r, w):
+        V(lambda v: v.tensor_copy(out, in_), r, w)
+
+    def tr(out, in_, r, w):
+        V(lambda v: v.transpose(out, in_), r, w)
+
+    def act(out, in_, f, bias, scale, r, w):
+        op("S", lambda s: s.activation(out, in_, f, bias=bias, scale=scale), r, w)
+
+    def mm(out, lhsT, rhs, start, stop, r, w):
+        op("P", lambda t: t.matmul(out, lhsT, rhs, start, stop), r, w)
+
+    B = lambda n, s: T[n + s]
+    st = {"A": 0, "B": 1}
+
+    dma("Y", T.W0I[:], T.w0[:], "dw", w=["W0I"])
+    dma("S", T.XO[:, 8:2056], T.x0[:, :], "dx", w=["XOb"])
+    for i in range(8):
+        dma("Y", T.ATI[16 * i:16 * i + 15, :], T.lk[16 * i:16 * i + 15, :], "dl", w=["ATI"])
+    dma("Y", T.ATI[15:128:16, :], T.nx[:, :], "dl", w=["ATI"])
+
+    def both(sem, src, keys):
+        for i in range(8):
+            o, a = (i % 2) * H + 8, 32 * (i // 2)
+            for par in range(2):
+                dma("SY"[par], T.X2[a + 16 * par:a + 16 * par + 16, o:o + 2048], src[16 * i:16 * i + 16, :], sem, keys, ["X2b"])
+    both("dy", T.x0, [])
+
+    def iota(out, pat, base, cm, key, flag=True):
+        if flag:
+            op("G", lambda q: q.iota(out, pat, base, cm, allow_small_or_imprecise_dtypes=True), w=[key])
+        else:
+            op("G", lambda q: q.iota(out, pat, base, cm), w=[key])
+    iota(T.PI[:, 0:1], [[1, 1]], 0, 1, "PI", False)
+    iota(T.Q[:], [[1, 144]], 0, 0, "Q")
+    iota(T.QG[:], [[1, 8], [0, 16]], 0, 0, "QG")
+    iota(T.QX2[:], [[0, 8], [1, 16]], 0, 0, "QX2")
+    iota(T.QX[:], [[0, 24], [1, 16]], 0, 0, "QX")
+    iota(T.DWL[:], [[16, 24]], 2816, 0, "DWL")
+    iota(T.QW[:, 0:256], [[32, 8], [0, 2], [1, 16]], 0, 0, "QW", False)
+    iota(T.QW[:, 256:512], [[32, 8], [0, 2], [1, 16]], 16, 0, "QW", False)
+    iota(T.QW[:, 512:768], [[1, 256]], 0, 0, "QW", False)
+    iota(T.NEWL[:], [[1, 384]], 2049, 0, "NEWL")
+    iota(T.IDT[:], [[1, 2816]], 0, 0, "IDT")
+    c = lambda i: T.C[:, i:i + 1]
+    V(lambda v: v.memset(T.ZR[:], 0.0), w=["ZR"])
+    for ph in range(2):
+        V(lambda v: v.memset(T.X2[:, ph * H:ph * H + 8], 255.0), w=["X2n"])
+        V(lambda v: v.memset(T.X2[:, ph * H + 2056:ph * H + H], 255.0), w=["X2n"])
+    V(lambda v: v.memset(T.XO[:, 0:8], 0.0), w=["XOn"])
+    V(lambda v: v.memset(T.XO[:, 2056:8 + NA], 0.0), w=["XOn"])
+    ts(T.PI[:, 1:2], T.PI[:, 0:1], 4, None, ALU.arith_shift_right, None, ["PI"], ["PI1"])
+    ts(T.PI[:, 2:3], T.PI[:, 0:1], 15, None, ALU.bitwise_and, None, ["PI"], ["PI2"])
+    ts(T.PI[:, 3:4], T.PI[:, 0:1], 4, 1, ALU.arith_shift_right, ALU.bitwise_and, ["PI"], ["PI3"])
+    ts(T.PI[:, 4:5], T.PI[:, 0:1], 1, None, ALU.bitwise_and, None, ["PI"], ["PI4"])
+    cp(T.C[:, 0:5], T.PI[:, 0:5], ["PI", "PI1", "PI2", "PI3", "PI4"], ["C0"])
+    for o, i, s1, s2, o0, o1, rr in [
+        (6, 2, 15.0, None, ALU.is_equal, None, []),
+        (7, 2, 14.0, None, ALU.is_equal, None, []),
+        (10, 2, 16.0, -209.0, ALU.mult, ALU.add, []),
+        (20, 4, -1.0, 1.0, ALU.mult, ALU.add, []),
+        (16, 3, 1000.0, c(0), ALU.mult, ALU.add, []),
+        (21, 3, -1000.0, 1000.0, ALU.mult, ALU.add, []),
+        (15, 2, -1.0, c(0), ALU.mult, ALU.add, []),
+        (8, 6, 1.0e6, 69.5, ALU.mult, ALU.add, [6]),
+        (22, 6, -16.0, c(2), ALU.mult, ALU.add, [6]),
+        (14, 6, 1.0, None, ALU.subtract, None, [6]),
+        (23, 6, -1.0, 1.0, ALU.mult, ALU.add, [6]),
+        (12, 20, -2.0, None, ALU.mult, None, [20]),
+        (13, 20, 15.0, None, ALU.mult, None, [20]),
+        (17, 16, 16.0, None, ALU.add, None, [16]),
+        (19, 21, c(0), None, ALU.add, None, [21]),
+        (24, 15, 15.0, None, ALU.add, None, [15]),
+        (9, 7, -1000.0, c(8), ALU.mult, ALU.add, [7, 8]),
+        (11, 22, 2.0, 4096.0, ALU.add, ALU.mult, [22]),
+        (18, 19, -16.0, None, ALU.add, None, [19]),
+    ]:
+        ts(c(o), c(i), s1, s2, o0, o1, ["C0"] + ["C%d" % x for x in rr], ["C%d" % o])
+    cp(T.VL0[:], T.W0I[:], ["W0I"], ["VLA", "VLB"])
+    for j, col in enumerate((16, 17, 18, 19)):
+        ts(T.SWB[:, 128 * j:128 * j + 128], T.Q[:, 0:128], c(col), None, ALU.is_equal, None, ["Q", "C%d" % col], ["SWB"])
+    swb = lambda s, d: T.SWB[:, 128 * (2 * s + d):128 * (2 * s + d) + 128]
+    swf = lambda s, d: T.SWF[:, 128 * (2 * s + d):128 * (2 * s + d) + 128]
+    ts(T.ID[:], T.Q[:, 0:128], c(0), None, ALU.is_equal, None, ["Q", "C0"], ["ID"])
+    ts(T.NI[:], T.Q[:, 0:128], c(0), -1.0, ALU.is_equal, ALU.mult, ["Q", "C0"], ["NI"])
+    ts(T.ZD[:], T.Q[:], c(24), None, ALU.is_equal, None, ["Q", "C24"], ["ZD"])
+    cp(T.SWF[:], T.SWB[:], ["SWB"], ["SWF"])
+    ts(T.DW[:], T.Q[:, 0:128], c(0), c(11), ALU.is_equal, ALU.mult, ["Q", "C0", "C11"], ["DW"])
+    ts(T.PN[:], T.Q[:, 0:128], c(0), 128.0, ALU.is_equal, ALU.mult, ["Q", "C0"], ["PN"])
+    ts(T.BK[:], T.QG[:], c(1), None, ALU.is_equal, None, ["QG", "C0"], ["BK"])
+    ts(T.T1[:], T.QX2[:], c(2), -16.0, ALU.is_lt, ALU.mult, ["QX2", "C0"], ["T1"])
+    ts(T.T2[:], T.T1[:], 1.0, c(23), ALU.add, ALU.mult, ["T1", "C23"], ["T2"])
+    tt(T.TU[:], T.T2[:], T.BK[:], ALU.mult, ["T2", "BK"], ["TU"])
+    ts(T.R1[:], T.QX[:], 0.0, None, ALU.is_gt, None, ["QX"], ["R1"])
+    V(lambda v: v.memset(T.AT[:, 2048:NA], -1.0), w=["AT"])
+
+    def late_constants():
+        ts(T.DIAG[:], T.QX[:], c(2), None, ALU.is_equal, None, ["QX", "C0"], ["DIAG"])
+        ts(T.TRI[:], T.QX[:], c(2), None, ALU.is_gt, None, ["QX", "C0"], ["TRI"])
+        ts(T.NEWL[:], T.NEWL[:], c(7), None, ALU.mult, None, ["NEWL", "C7"], ["NEWL"])
+        ts(T.DWL[:], T.DWL[:], c(2), None, ALU.add, None, ["DWL", "C0"], ["DWL"])
+        ts(T.QW[:], T.QW[:], 127, None, ALU.bitwise_and, None, ["QW"], ["QW"])
+        ts(T.W3[:], T.QW[:], c(0), None, ALU.is_equal, None, ["QW", "C0"], ["W3"])
+
+    sl = lambda s: slice(12 * st[s], 12 * st[s] + 12)
+    sw = lambda s: slice(192 * st[s], 192 * st[s] + 192)
+    X2ALL, XOALL = ["X2b", "X2n"], ["XOb", "XOn"]
+
+    def vx_lists(s, src, key):
+        for u in range(2):
+            o = 12 * st[s] + 6 * u
+            ts(T.VX0[:, o:o + 6], src(u), 8.0, None, ALU.add, None, [key], ["VX" + s])
+
+    for s in "AB":
+        vx_lists(s, lambda u: T.W0I[:, 12 * st[s] + u:12 * st[s] + 12:2], "W0I")
+    cp(T.AT[:, 0:2048], T.ATI[:], ["ATI"], ["AT"])
+
+    def agather(s, key=True):
+        act(T.GA[:, sw(s)], T.AT[:].indirect(T.VL0[:, sl(s)]), ACT.Identity, 0.0, 1.0, ["AT", "VL" + s], ["GA" + s])
+        if key:
+            dma("Y", T.GA3[:, sl(s), :], T.GA[:, sw(s)], "dg" + s, ["GA" + s], ["G3" + s])
+
+    def xgather(s):
+        act(T.XV[:, sw(s)], T.XO[:].indirect(T.VX0[:, sl(s)]), ACT.Identity, 0.0, 1.0, XOALL + ["VX" + s], ["XV" + s])
+
+    def swap4(out, o0, mat, src, key, r, stop, n=1):
+        k = 0
+        for rep in range(n):
+            for u in range(2):
+                for v in range(2):
+                    k += 1
+                    mm(out[:, o0 + v:o0 + 12:2, :], mat(v, u), src(u), False, stop and k == 4 * n, r, [key])
+
+    def xv(s):
+        return lambda u: T.XV[:, 192 * st[s] + 96 * u:192 * st[s] + 96 * u + 96]
+
+    def zswap(s, first):
+        o = B("pZ", s)
+        if first:
+            mm(o[:, 0:12, :], T.ZR[:], T.XV[:, sw(s)], True, False, ["ZR", "XV" + s], ["pZ" + s])
+        else:
+            mm(o[:, 0:12, :], T.ID[:], B("Z", s)[:, 0:192], True, False, ["ID", "Z" + s], ["pZ" + s])
+        swap4(o, 0, swb, xv(s), "pZ" + s, ["XV" + s, "SWB"], True, 2 if first else 1)
+
+    def zact(s, first, final=False):
+        bias = 127.75 if first else 63.75
+        src = B("pZ", s)[:, 0:12, :]
+        if final:
+            act(B("ZF", s)[:], src, ACT.Identity, bias, 0.5, ["pZ" + s], ["ZF" + s])
+        else:
+            for d in range(2):
+                act(B("Z", s)[:, 192 * d:192 * d + 192], src, ACT.Identity, bias, 0.5, ["pZ" + s], ["Z" + s])
+
+    def lists(s, L):
+        lt, cl = B("LT", s), B("CL", s)
+        for b in range(6):
+            o = 192 * st[s] + 32 * b
+            tr(lt[:, b:192:6], T.GA[:, o:o + 32], ["GA" + s], ["LT" + s])
+        for g2 in range(2):
+            ts(cl[:, g2:12 * L:2], lt[:, 96 * g2:96 * g2 + 6 * L], 8.0 + H * g2, None, ALU.add, None, ["LT" + s], ["CL" + s])
+
+    def gakey(s):
+        o = B("pK", s)
+        mm(o[:, 0:12, :], T.ZR[:], B("Z", s)[:, 0:192], True, False, ["ZR", "Z" + s], ["pK" + s])
+        swap4(o, 0, swf, lambda u: T.GA3[:, 12 * st[s] + u:12 * st[s] + 12:2, :], "pK" + s, ["G3" + s, "SWF"], False)
+
+    def valid(s, t):
+        thr = 8 if t else 9
+        act(B("VAL", s)[:], B("pD", s)[:, 0:192], ACT.Sign, c(thr), -1.0, ["pD" + s, "C%d" % thr], ["VAL" + s])
+
+    def keymm(s):
+        mm(B("pK", s)[:, 0:12, :], T.DW[:], B("VAL", s)[:], False, True, ["DW", "VAL" + s], ["pK" + s])
+
+    def umm(s, k):
+        o = B("pZ", s)[:, 12:24, :]
+        mm(o, T.TU[:], B("VAL", s)[:], True, k == 0, ["TU", "VAL" + s], ["pZ" + s])
+        if k:
+            mm(o, T.ID[:], B("F", s)[:], False, True, ["ID", "F" + s], ["pZ" + s])
+
+    def frelu(s):
+        act(B("F", s)[:], B("pZ", s)[:, 12:24, :], ACT.Relu, c(10), 1.0, ["pZ" + s, "C10"], ["F" + s])
+
+    def decode(s, last):
+        kt, sc, vi, vj = B("KT", s), B("SC", s), B("VI", s), B("VJ", s)
+        tr(kt[:], B("pK", s)[:, 0:12, :], ["pK" + s], ["KT" + s])
+        V(lambda v: v.tensor_tensor_scan(sc[:], T.R1[:, 0:192], kt[:], 0.0, ALU.mult, ALU.max), ["R1", "KT" + s], ["SC" + s])
+        cp(vi[:], sc[:, 15:192:16], ["SC" + s], ["VI" + s])
+        ts(vj[:], vi[:], 4095, None, ALU.bitwise_and, None, ["VI" + s], ["VJ" + s])
+        cp(T.VL0[:, sl(s)], vj[:], ["VJ" + s], ["VL" + s])
+        vx_lists(s, lambda u: vj[:, u:12:2], "VJ" + s)
+        if last:
+            cp(T.VLF[:, sl(s)], vj[:], ["VJ" + s], ["VLF" + s])
+            ts(T.VXN[:, sl(s)], vj[:], 8.0, None, ALU.add, None, ["VJ" + s], ["VXN" + s])
+
+    def b_gather(s):
+        act(B("XG", s)[:], T.X2[:].indirect(B("CL", s)[:, 0:24]), ACT.Identity, 0.0, 1.0, X2ALL + ["CL" + s], ["XG" + s])
+
+    def b_sub(s):
+        o = B("pS", s)[:, 0:24, :]
+        mm(o, T.ID[:], B("XG", s)[:], True, False, ["ID", "XG" + s], ["pS" + s])
+        mm(o, T.NI[:], B("Z", s)[:], False, True, ["NI", "Z" + s], ["pS" + s])
+
+    def b_abs(s):
+        act(B("AB", s)[:, 0:384], B("pS", s)[:, 0:24, :], ACT.Abs, 128.0, 1.0, ["pS" + s], ["AB%s0" % s, "AB%s1" % s])
+
+    def vgather(s, i, n):
+        tt(B("CD", s)[:, 192 * i:192 * (i + n)], T.X2[:].indirect(B("CL", s)[:, 12 * i:12 * (i + n)]),
+           B("Z", s)[:, 0:192 * n], ALU.subtract, X2ALL + ["CL" + s, "Z" + s], ["CD%s%d" % (s, x) for x in range(i, i + n)])
+
+    def vabs(s, i, n):
+        act(B("AB", s)[:, 192 * i:192 * (i + n)], B("CD", s)[:, 192 * i:192 * (i + n)], ACT.Abs, 128.0, 1.0,
+            ["CD%s%d" % (s, x) for x in range(i, i + n)], ["AB%s%d" % (s, x) for x in range(i, i + n)])
+
+    def dist(s, i, n, L, start):
+        for x in range(i, i + n):
+            mm(B("pD", s)[:, 0:192], T.ZD[:, 15 - x:143 - x], B("AB", s)[:, 192 * x:192 * x + 192], start and x == i,
+               x == L - 1, ["ZD", "AB%s%d" % (s, x)], ["pD" + s])
+
+    def begin(s, L):
+        agather(s)
+        xgather(s)
+        zswap(s, True)
+        zact(s, True)
+        lists(s, L)
+
+    def period(sel, k, blk, kb, t):
+        L = 14 + t
+        last = k == 3
+        if blk:
+            b_gather(blk)
+            vgather(blk, 2, 2)
+            vgather(blk, 4, 2)
+        if sel:
+            valid(sel, t)
+        if blk:
+            b_sub(blk)
+        if sel:
+            keymm(sel)
+            if not last:
+                umm(sel, k)
+        if blk:
+            b_abs(blk)
+        elif not t:
+            late_constants()
+        if sel:
+            decode(sel, last)
+        if blk:
+            vabs(blk, 2, 4)
+            if kb:
+                mm(B("pD", blk)[:, 0:192], T.PN[:], B("F", blk)[:], True, False, ["PN", "F" + blk], ["pD" + blk])
+            dist(blk, 0, 6, L, not kb)
+        if sel:
+            if not last:
+                frelu(sel)
+                agather(sel)
+            xgather(sel)
+        if blk:
+            vgather(blk, 6, 2)
+            vgather(blk, 8, 2)
+        if sel:
+            zswap(sel, False)
+            if last:
+                diff(sel)
+            zact(sel, False, last)
+            if not last:
+                lists(sel, L)
+            elif not t:
+                agather(sel, False)
+        if blk:
+            vabs(blk, 6, 4)
+            gakey(blk)
+            dist(blk, 6, 4, L, False)
+            vgather(blk, 10, 2)
+            vgather(blk, 12, 2)
+            if L == 15:
+                vgather(blk, 14, 1)
+        if sel and last:
+            votes(sel, t)
+        if blk:
+            vabs(blk, 10, L - 10)
+            dist(blk, 10, L - 10, L, False)
+
+    def diff(s):
+        o = B("pS", s)
+        mm(o[:, 0:12, :], T.NI[:], B("Z", s)[:, 0:192], True, False, ["NI", "Z" + s], ["pS" + s])
+        swap4(o, 0, swb, xv(s), "pS" + s, ["XV" + s, "SWB"], True)
+
+    def votes(s, t):
+        ts(B("GT", s)[:], B("pS", s)[:, 0:12, :], -128.0, None, ALU.is_gt, None, ["pS" + s], ["GT" + s])
+        o = B("pZ", s)
+        mm(o[:, 12:24, :], T.ZR[:], B("ZF", s)[:], True, False, ["ZR", "ZF" + s], ["pZ" + s])
+        swap4(o, 12, swb, lambda u: B("ZF", s)[:, u:12:2, :], "pZ" + s, ["ZF" + s, "SWB"], True)
+        mm(B("pK", s)[:, 0:12, :], T.BK[:], B("GT", s)[:], True, True, ["BK", "GT" + s], ["pK" + s])
+        zn = "ZN%d" % t
+        act(T[zn][:, sw(s)], o[:, 12:24, :], ACT.Identity, 0.0, 1.0, ["pZ" + s], [zn + s])
+        act(T.VF[:, sw(s)], T.IDT[:].indirect(T.VL0[:, sl(s)]), ACT.Identity, 0.0, 1.0, ["IDT", "VL" + s], ["VF" + s])
+        tr(B("KT", s)[:], B("pK", s)[:, 0:12, :], ["pK" + s], ["KT" + s])
+        ts(T.WT[:, sl(s)], B("KT", s)[:, 0:192:16], 9.0, EPS, ALU.is_lt, ALU.add, ["KT" + s], ["WT" + s])
+        for d in range(2):
+            cp(T.VB[:, 24 * d + 12 * st[s]:24 * d + 12 * st[s] + 12, :], T.VF[:, sw(s)], ["VF" + s], ["VB" + s])
+        wait_for("G", [zn + s], [])
+        trs = []
+        for q in range(4 * st[s], 4 * st[s] + 4):
+            if q == rank:
+                continue
+            dst = T.cores[q]
+            rid, pid, _e = topo.addr(dst)
+            j = 2 * len(trs)
+            mask = sum(1 << e for e in topo.engines(core, dst)[j:j + 2])
+            trs.append(RemoteDMATransfer(dst_ids=[DstId(rid=rid, pnc=pid)], dma_engine_mask=mask, remote_sem=T.sem["arr%d" % t],
+                                         src=T[zn][:, 48 * q:48 * q + 48], dst=T["RZ%d" % t][:, 48 * rank:48 * rank + 48]))
+        g.remote_dma_fused(trs, local_sem=T.sem.lsem)
+
+    def flips(t):
+        all_, ear = T.pKA, T.pKB
+        act(T.XW[:], T.XO[:].indirect(T.VXN[:]), ACT.Identity, 0.0, 1.0, XOALL + ["VXNA", "VXNB"], ["XW"])
+        mm(ear[:, 0:24, :], T.ZR[:], T["ZN%d" % t][:], True, False, ["ZR", "ZN%dA" % t, "ZN%dB" % t], ["pKB"])
+        for b in range(24):
+            e0 = 24 * b
+            ts(T.E[:, e0:e0 + 24, :], T.VB[:, b:b + 24, :], T.VLF[:, b:b + 1], T.WT[:, b:b + 1], ALU.is_equal, ALU.mult,
+               ["VBA", "VBB", "VLFA", "VLFB", "WTA", "WTB"], ["E%d" % b])
+            mm(all_[:, b:24, :], T.BK[:], T.E[:, e0:e0 + 24 - b, :], b == 0, False, ["BK", "E%d" % b], ["pKA"])
+            if b:
+                mm(all_[:, 0:b, :], T.BK[:], T.E[:, e0 + 24 - b:e0 + 24, :], False, b == 23, ["BK", "E%d" % b], ["pKA"])
+            if b < 23:
+                mm(ear[:, b + 1:24, :], T.BK[:], T.E[:, e0 + 1:e0 + 24 - b, :], False, False, ["BK", "E%d" % b], ["pKB"])
+        tt(T.DG[:], T.E[:, 0:576:24, :], T.TRI[:], ALU.mult, ["E%d" % b for b in range(24)] + ["TRI"], ["DG"])
+        mm(ear[:, 0:24, :], T.BK[:], T.DG[:], False, True, ["BK", "DG"], ["pKB"])
+        ts(T.DX[:], T.XW[:], c(12), c(13), ALU.mult, ALU.add, ["XW", "C12", "C13"], ["DX"])
+        ts(T.FL[:], all_[:, 0:24, :], 1.0, None, ALU.is_lt, None, ["pKA"], ["FL"])
+        tt(T.S3[:], T.DWL[:], T.VLF[:], ALU.subtract, ["DWL", "VLFA", "VLFB"], ["S3"])
+        tt(T.DM[:], ear[:, 0:24, :], T.DIAG[:], ALU.mult, ["pKB", "DIAG"], ["DM"])
+        tt(T.FX[:], T.FL[:], T.DX[:], ALU.mult, ["FL", "DX"], ["FX"])
+        V(lambda v: v.tensor_tensor_scan(T.SC2[:], T.R1[:], T.DM[:], 0.0, ALU.mult, ALU.add), ["R1", "DM"], ["SC2"])
+        ts(T.S1[:], T.SC2[:, 15:384:16], 0.0, None, ALU.is_gt, None, ["SC2"], ["S1"])
+        tt(T.S2[:], T.S1[:], T.S3[:], ALU.mult, ["S1", "S3"], ["S2"])
+        tt(T.S4[:], T.S2[:], T.VLF[:], ALU.add, ["S2", "VLFA", "VLFB"], ["S4"])
+        ts(T.XOFF[:], T.S4[:], 8.0, None, ALU.add, None, ["S4"], ["XOFF"])
+        ga = ["GAA", "GAB"]
+        if not t:
+            cp(T.AOFF[:], T.S4[:], ["S4"], ["AOFF"])
+            ts(T.AT[:, 2048:2432], T.GA[:], c(6), c(14), ALU.mult, ALU.add, ga + ["C6", "C14"], ["AT"])
+        tt(T.XO[:].indirect(T.XOFF[:]), T.XW[:], T.FX[:], ALU.add, ["XW", "FX", "XOFF"], XOALL)
+        if not t:
+            tt(T.AT[:].indirect(T.AOFF[:]), T.GA[:], T.NEWL[:], ALU.add, ga + ["NEWL", "AOFF", "AT"], ["AT"])
+            both("dd", T.XO[:, 8:2056], XOALL)
+
+    def arrivals(t):
+        rz, zn = "RZ%d" % t, "ZN%d" % t
+        arrive("arr%d" % t, 14, rz)
+        for ph, pk in ((0, "pSA"), (1, "pSB"), (2, "pZB"))[2 * t:]:
+            for r in range(8):
+                d = (rank - r) % 8
+                if ph == 2:
+                    o = 512 + 128 - 16 * d
+                else:
+                    e = (ph - d) % 2
+                    o = 256 * e + 32 * ((((ph - d) % 8 - e) // 2) % 4)
+                src, keys = (T[zn], [zn + "A", zn + "B"]) if r == rank else (T[rz], [rz])
+                mm(T[pk][:, 3 * r:3 * r + 3, :], T.W3[:, o:o + 128], src[:, 48 * r:48 * r + 48], True, True, ["W3"] + keys, [pk])
+            n = 8 + 2048 + 384 * t
+            if ph == 2:
+                act(T.XO[:, n:n + 384], T[pk][:, 0:24, :], ACT.Identity, -128.0, 1.0, [pk], ["XOn"])
+            else:
+                act(T.X2[:, ph * H + n:ph * H + n + 384], T[pk][:, 0:24, :], ACT.Identity, -128.0, 1.0, [pk], ["X2n"])
+
+    for t in range(2):
+        L = 14 + t
+        begin("A", L)
+        begin("B", L)
+        if t:
+            arrivals(0)
+        period(None, -1, "A", 0, t)
+        for k in range(4):
+            period("A", k, "B", k, t)
+            period("B", k, "A" if k < 3 else None, k + 1, t)
+        if t:
+            dma("Y", T.yv[:, :], T.VF[0:128:16, :], "dv", r=["VFA", "VFB"])
+        flips(t)
+    arrivals(1)
+    dma("Y", T.yx[:, :], T.XO[:, 8:2824], "do", r=XOALL)
+    finish()
+    g.wait_ge(T.sem.lsem, 28)

@@ -6,6 +6,11 @@ ACT = ActivationFunctionType
 H = 8 + 2816
 NA = 2816 + 384
 EPS = 2.0 ** -9
+NB = 1
+ABS = ((2, 2), (4, 2), (6, 4), (10, 2), (12, 3))
+ORDER = (2, 4, 0, 6, 8, 10, 12)
+CY, FV, FS, FP, PE, WAKE = 0.83e-3, 0.06, 0.07, 0.04, 0.45e-3, 0.08
+GA_C, SC_C = 1.5, 3.5
 
 SCRATCH = {}
 
@@ -19,10 +24,10 @@ _decl("bfloat16", X2=[2 * H], XO=[8 + NA], W3=[768], ZD=[144], BK=[128], ID=[128
       ZR=[128], SWB=[512], R1=[384], DIAG=[24, 16], TRI=[24, 16], E=[576, 16], DG=[24, 16], DX=[384], FX=[384], FL=[384],
       XV=[384], XW=[384], ZN0=[384], ZN1=[384], RZ0=[384], RZ1=[384])
 _decl("float32", AT=[NA], IDT=[2816], C=[32], Q=[144], QX=[24, 16], QX2=[128], QG=[128], T1=[128], T2=[128], SWF=[512],
-      NEWL=[384], DWL=[24], VLF=[24], WT=[24], VF=[384], DM=[384], SC2=[384], S1=[24], S2=[24], S3=[24], S4=[24],
-      GA=[384], GA3=[24, 16])
+      NEWL=[384], DWL=[24], VLF=[24], WT=[24], VF=[384], DM=[384], SC2=[384], RS=[24, 16], RT=[384], S1=[24], S2=[24], S3=[24],
+      S4=[24], GA=[384], GA3=[24, 16])
 _decl("int32", ATI=[2048], W0I=[24], PI=[8], QW=[768])
-_decl("uint16", VL0=[24], VX0=[24], VXN=[24], VB=[48, 16], AOFF=[24], XOFF=[24])
+_decl("uint16", VL0=[24], VX0=[24], VXN=[24], VB=[49, 16], AOFF=[24], XOFF=[24])
 for _s in "AB":
     _decl("bfloat16", **{"CD" + _s: [3072], "AB" + _s: [3072], "XG" + _s: [384], "Z" + _s: [384], "ZF" + _s: [12, 16],
                          "VAL" + _s: [192], "F" + _s: [192], "GT" + _s: [192]})
@@ -33,14 +38,68 @@ for _s in "AB":
 SEMAPHORES = ["sv", "ss", "sp", "sg", "dw", "dl", "dx", "dy", "dd", "do", "dv", "dgA", "dgB", "arr0", "arr1", "lsem"]
 
 
-def make_emitter(g, T):
+def schedule(ops):
+    preds, lastw, readers = [], {}, {}
+    for j, o in enumerate(ops):
+        p = {}
+        for k in o["r"]:
+            if k in lastw:
+                p[lastw[k]] = 0 if k[0] == "p" and ops[lastw[k]]["e"] == o["e"] else 1
+            if k[0] == "p":
+                for x in readers.get(k, ()):
+                    p.setdefault(x, 0 if ops[x]["e"] == o["e"] else 1)
+        for k in o["w"]:
+            for x in ([lastw[k]] if k in lastw else []) + readers.get(k, []):
+                same = ops[x]["e"] == o["e"] or (o["sem"] and ops[x]["sem"] == o["sem"])
+                p.setdefault(x, 0 if same else 1)
+        p.pop(j, None)
+        preds.append(p)
+        for k in o["r"]:
+            readers.setdefault(k, []).append(j)
+        for k in o["w"]:
+            lastw[k] = j
+            readers[k] = []
+    n = len(ops)
+    succ = [[] for _ in range(n)]
+    for j in range(n):
+        for i in preds[j]:
+            succ[i].append(j)
+    bl = [0.0] * n
+    for j in range(n - 1, -1, -1):
+        bl[j] = ops[j]["c"] + ops[j]["lat"] + max([bl[x] + WAKE for x in succ[j]] or [0.0])
+    left = [len(preds[j]) for j in range(n)]
+    base = [0.0] * n
+    free, out = {}, []
+    ready = [j for j in range(n) if not left[j]]
+    dmaq = 0.0
+    while ready:
+        st = [max(base[j], free.get(ops[j]["e"], 0.0)) for j in ready]
+        t0 = min(st) + 0.02
+        j = max((bl[x], -x, x) for x, s in zip(ready, st) if s <= t0)[2]
+        ready.remove(j)
+        o = ops[j]
+        s = max(base[j], free.get(o["e"], 0.0))
+        fin = free[o["e"]] = s + o["c"]
+        if o["lat"]:
+            dmaq = max(dmaq, fin) + o["by"]
+            fin = max(dmaq, fin) + o["lat"]
+        out.append(o)
+        for x in succ[j]:
+            base[x] = max(base[x], fin + WAKE if preds[x][j] else s + o["c"])
+            left[x] -= 1
+            if not left[x]:
+                ready.append(x)
+    return out
+
+
+def emit(g, T, ops):
     eng = {"V": g.vector, "S": g.scalar, "P": g.tensor, "G": g, "Y": g.sync}
     sem = {"V": "sv", "S": "ss", "P": "sp", "G": "sg"}
     cnt = {}
     know = {e: {} for e in eng}
     lastw, readers, snaps = {}, {}, {}
 
-    def wait_for(e, r, w):
+    def wait_for(e, r, w, me):
         need = []
         for k in r:
             if k in lastw:
@@ -53,7 +112,7 @@ def make_emitter(g, T):
             need.extend((x, True) for x in readers.get(k, ()))
         mx = {}
         for (s, c), anti in need:
-            if s == e and (anti or e == "P"):
+            if (s == e and (anti or e == "P")) or s == me:
                 continue
             if s not in eng:
                 c = cnt[s]
@@ -70,12 +129,26 @@ def make_emitter(g, T):
                     know[e][s2] = max(know[e].get(s2, 0), c2)
                 know[e][s] = max(know[e].get(s, 0), c)
 
-    def note(tok, e, r, w):
+    for o in ops:
+        e, r, w = o["e"], o["r"], o["w"]
+        if e == "R":
+            cnt[o["sem"]] = 14
+            for k in w:
+                lastw[k] = (o["sem"], 14)
+            continue
+        wait_for(e, r, w, o["sem"])
+        if o["sem"] == "lsem":
+            o["fn"](eng[e])
+            continue
+        s, add = (o["sem"], 16) if o["sem"] else (e, 1)
+        cnt[s] = cnt.get(s, 0) + add
+        o["fn"](eng[e]).then_inc(T.sem[sem.get(s, s)], add)
+        tok = (s, cnt[s])
         sn = dict(know[e])
-        if tok[0] in eng:
-            sn[tok[0]] = tok[1]
+        if s in eng:
+            sn[s] = cnt[s]
         else:
-            for s2, c2 in snaps.get((tok[0], tok[1] - 16), {}).items():
+            for s2, c2 in snaps.get((s, cnt[s] - 16), {}).items():
                 sn[s2] = max(sn.get(s2, 0), c2)
         snaps[tok] = sn
         for k in r:
@@ -83,99 +156,90 @@ def make_emitter(g, T):
         for k in w:
             lastw[k] = tok
             readers[k] = []
-
-    def op(e, fn, r=(), w=()):
-        wait_for(e, r, w)
-        cnt[e] = cnt.get(e, 0) + 1
-        fn(eng[e]).then_inc(T.sem[sem[e]], 1)
-        note((e, cnt[e]), e, r, w)
-
-    def dma(e, out, in_, s, r=(), w=()):
-        wait_for(e, r, w)
-        cnt[s] = cnt.get(s, 0) + 16
-        eng[e].dma_start(out=out, in_=in_).then_inc(T.sem[s], 16)
-        note((s, cnt[s]), e, r, w)
-
-    def arrive(s, c, key):
-        cnt[s] = c
-        lastw[key] = (s, c)
-
-    def finish():
-        for s, c in sorted(cnt.items()):
-            if know["G"].get(s, 0) < c:
-                g.wait_ge(T.sem[sem.get(s, s)], c)
-    return op, dma, arrive, finish, wait_for
+    for s, c in sorted(cnt.items()):
+        if know["G"].get(s, 0) < c:
+            g.wait_ge(T.sem[sem.get(s, s)], c)
+    g.wait_ge(T.sem.lsem, 28)
 
 
 def rank_program(g, core, T, topo):
     rank = T.rank_of(core)
     if rank is None:
         return
-    op, dma, arrive, finish, wait_for = make_emitter(g, T)
+    ops = []
 
-    def V(fn, r=(), w=()):
-        op("V", fn, r, w)
+    def op(e, fn, r, w, c, sem=None, lat=0.0, by=0.0):
+        ops.append({"e": e, "fn": fn, "r": list(r), "w": list(w), "c": c, "sem": sem, "lat": lat, "by": by})
 
-    def ts(out, in0, s1, s2, op0, op1, r, w):
+    def V(fn, r, w, n):
+        op("V", fn, r, w, FV + max(64, n) * CY)
+
+    def ts(out, in0, s1, s2, op0, op1, r, w, n=64):
         if op1 is None:
-            V(lambda v: v.tensor_scalar(out, in0, s1, None, op0), r, w)
+            V(lambda v: v.tensor_scalar(out, in0, s1, None, op0), r, w, n)
         else:
-            V(lambda v: v.tensor_scalar(out, in0, s1, s2, op0, op1), r, w)
+            V(lambda v: v.tensor_scalar(out, in0, s1, s2, op0, op1), r, w, n)
 
-    def tt(out, in0, in1, o, r, w):
-        V(lambda v: v.tensor_tensor(out, in0, in1, o), r, w)
+    def tt(out, in0, in1, o, r, w, n=64):
+        V(lambda v: v.tensor_tensor(out, in0, in1, o), r, w, n)
 
-    def cp(out, in_, r, w):
-        V(lambda v: v.tensor_copy(out, in_), r, w)
+    def cp(out, in_, r, w, n=64):
+        V(lambda v: v.tensor_copy(out, in_), r, w, n)
 
-    def tr(out, in_, r, w):
-        V(lambda v: v.transpose(out, in_), r, w)
+    def tr(out, in_, r, w, n=64):
+        V(lambda v: v.transpose(out, in_), r, w, n)
 
-    def act(out, in_, f, bias, scale, r, w):
-        op("S", lambda s: s.activation(out, in_, f, bias=bias, scale=scale), r, w)
+    def ms(ap, x, w, n=64):
+        V(lambda v: v.memset(ap, x), [], w, n)
 
-    def mm(out, lhsT, rhs, start, stop, r, w):
-        op("P", lambda t: t.matmul(out, lhsT, rhs, start, stop), r, w)
+    def act(out, in_, f, bias, scale, r, w, n):
+        op("S", lambda s: s.activation(out, in_, f, bias=bias, scale=scale), r, w, FS + n * CY)
+
+    def mm(out, lhsT, rhs, start, stop, r, w, n):
+        op("P", lambda t: t.matmul(out, lhsT, rhs, start, stop), r, w, FP + max(64, n) * PE)
+
+    def dma(e, out, in_, sem, r, w, kb):
+        op(e, lambda q: q.dma_start(out=out, in_=in_), r, w, 0.07, sem, 2.0, kb / 200.0)
 
     B = lambda n, s: T[n + s]
     st = {"A": 0, "B": 1}
 
-    dma("Y", T.W0I[:], T.w0[:], "dw", w=["W0I"])
-    dma("S", T.XO[:, 8:2056], T.x0[:, :], "dx", w=["XOb"])
+    dma("Y", T.W0I[:], T.w0[:], "dw", [], ["W0I"], 12)
     for i in range(8):
-        dma("Y", T.ATI[16 * i:16 * i + 15, :], T.lk[16 * i:16 * i + 15, :], "dl", w=["ATI"])
-    dma("Y", T.ATI[15:128:16, :], T.nx[:, :], "dl", w=["ATI"])
+        dma("Y", T.ATI[16 * i:16 * i + 15, :], T.lk[16 * i:16 * i + 15, :], "dl", [], ["ATI"], 120)
+    dma("Y", T.ATI[15:128:16, :], T.nx[:, :], "dl", [], ["ATI"], 64)
+    dma("Y", T.XO[:, 8:2056], T.x0[:, :], "dx", [], ["XOb"], 512)
 
     def both(sem, src, keys):
         for i in range(8):
             o, a = (i % 2) * H + 8, 32 * (i // 2)
             for par in range(2):
-                dma("SY"[par], T.X2[a + 16 * par:a + 16 * par + 16, o:o + 2048], src[16 * i:16 * i + 16, :], sem, keys, ["X2b"])
+                dma("Y", T.X2[a + 16 * par:a + 16 * par + 16, o:o + 2048], src[16 * i:16 * i + 16, :], sem, keys, ["X2b"], 64)
     both("dy", T.x0, [])
 
-    def iota(out, pat, base, cm, key, flag=True):
+    def iota(out, pat, base, cm, key, n, flag=True):
         if flag:
-            op("G", lambda q: q.iota(out, pat, base, cm, allow_small_or_imprecise_dtypes=True), w=[key])
+            op("G", lambda q: q.iota(out, pat, base, cm, allow_small_or_imprecise_dtypes=True), [], [key], 0.13 + 2 * n * CY)
         else:
-            op("G", lambda q: q.iota(out, pat, base, cm), w=[key])
-    iota(T.PI[:, 0:1], [[1, 1]], 0, 1, "PI", False)
-    iota(T.Q[:], [[1, 144]], 0, 0, "Q")
-    iota(T.QG[:], [[1, 8], [0, 16]], 0, 0, "QG")
-    iota(T.QX2[:], [[0, 8], [1, 16]], 0, 0, "QX2")
-    iota(T.QX[:], [[0, 24], [1, 16]], 0, 0, "QX")
-    iota(T.DWL[:], [[16, 24]], 2816, 0, "DWL")
-    iota(T.QW[:, 0:256], [[32, 8], [0, 2], [1, 16]], 0, 0, "QW", False)
-    iota(T.QW[:, 256:512], [[32, 8], [0, 2], [1, 16]], 16, 0, "QW", False)
-    iota(T.QW[:, 512:768], [[1, 256]], 0, 0, "QW", False)
-    iota(T.NEWL[:], [[1, 384]], 2049, 0, "NEWL")
-    iota(T.IDT[:], [[1, 2816]], 0, 0, "IDT")
+            op("G", lambda q: q.iota(out, pat, base, cm), [], [key], 0.13 + 2 * n * CY)
+    iota(T.PI[:, 0:1], [[1, 1]], 0, 1, "PI", 1, False)
+    iota(T.Q[:], [[1, 144]], 0, 0, "Q", 144)
+    iota(T.QG[:], [[1, 8], [0, 16]], 0, 0, "QG", 128)
+    iota(T.QX2[:], [[0, 8], [1, 16]], 0, 0, "QX2", 128)
+    iota(T.QX[:], [[0, 24], [1, 16]], 0, 0, "QX", 384)
+    iota(T.DWL[:], [[16, 24]], 2816, 0, "DWL", 24)
+    iota(T.QW[:, 0:256], [[32, 8], [0, 2], [1, 16]], 0, 0, "QW", 256, False)
+    iota(T.QW[:, 256:512], [[32, 8], [0, 2], [1, 16]], 16, 0, "QW", 256, False)
+    iota(T.QW[:, 512:768], [[1, 256]], 0, 0, "QW", 256, False)
+    iota(T.NEWL[:], [[1, 384]], 2049, 0, "NEWL", 384)
+    iota(T.IDT[:], [[1, 2816]], 0, 0, "IDT", 2816)
     c = lambda i: T.C[:, i:i + 1]
-    V(lambda v: v.memset(T.ZR[:], 0.0), w=["ZR"])
+    ms(T.ZR[:], 0.0, ["ZR"])
     for ph in range(2):
-        V(lambda v: v.memset(T.X2[:, ph * H:ph * H + 8], 255.0), w=["X2n"])
-        V(lambda v: v.memset(T.X2[:, ph * H + 2056:ph * H + H], 255.0), w=["X2n"])
-    V(lambda v: v.memset(T.XO[:, 0:8], 0.0), w=["XOn"])
-    V(lambda v: v.memset(T.XO[:, 2056:8 + NA], 0.0), w=["XOn"])
+        ms(T.X2[:, ph * H:ph * H + 8], 255.0, ["X2n"])
+        ms(T.X2[:, ph * H + 2056:ph * H + H], 255.0, ["X2n"], 384)
+    ms(T.XO[:, 0:8], 0.0, ["XOn"])
+    ms(T.XO[:, 2056:8 + NA], 0.0, ["XOn"], 576)
     ts(T.PI[:, 1:2], T.PI[:, 0:1], 4, None, ALU.arith_shift_right, None, ["PI"], ["PI1"])
     ts(T.PI[:, 2:3], T.PI[:, 0:1], 15, None, ALU.bitwise_and, None, ["PI"], ["PI2"])
     ts(T.PI[:, 3:4], T.PI[:, 0:1], 4, 1, ALU.arith_shift_right, ALU.bitwise_and, ["PI"], ["PI3"])
@@ -205,29 +269,27 @@ def rank_program(g, core, T, topo):
         ts(c(o), c(i), s1, s2, o0, o1, ["C0"] + ["C%d" % x for x in rr], ["C%d" % o])
     cp(T.VL0[:], T.W0I[:], ["W0I"], ["VLA", "VLB"])
     for j, col in enumerate((16, 17, 18, 19)):
-        ts(T.SWB[:, 128 * j:128 * j + 128], T.Q[:, 0:128], c(col), None, ALU.is_equal, None, ["Q", "C%d" % col], ["SWB"])
+        ts(T.SWB[:, 128 * j:128 * j + 128], T.Q[:, 0:128], c(col), None, ALU.is_equal, None, ["Q", "C%d" % col], ["SWB"], 128)
     swb = lambda s, d: T.SWB[:, 128 * (2 * s + d):128 * (2 * s + d) + 128]
     swf = lambda s, d: T.SWF[:, 128 * (2 * s + d):128 * (2 * s + d) + 128]
-    ts(T.ID[:], T.Q[:, 0:128], c(0), None, ALU.is_equal, None, ["Q", "C0"], ["ID"])
-    ts(T.NI[:], T.Q[:, 0:128], c(0), -1.0, ALU.is_equal, ALU.mult, ["Q", "C0"], ["NI"])
-    ts(T.ZD[:], T.Q[:], c(24), None, ALU.is_equal, None, ["Q", "C24"], ["ZD"])
-    cp(T.SWF[:], T.SWB[:], ["SWB"], ["SWF"])
-    ts(T.DW[:], T.Q[:, 0:128], c(0), c(11), ALU.is_equal, ALU.mult, ["Q", "C0", "C11"], ["DW"])
-    ts(T.PN[:], T.Q[:, 0:128], c(0), 128.0, ALU.is_equal, ALU.mult, ["Q", "C0"], ["PN"])
-    ts(T.BK[:], T.QG[:], c(1), None, ALU.is_equal, None, ["QG", "C0"], ["BK"])
-    ts(T.T1[:], T.QX2[:], c(2), -16.0, ALU.is_lt, ALU.mult, ["QX2", "C0"], ["T1"])
-    ts(T.T2[:], T.T1[:], 1.0, c(23), ALU.add, ALU.mult, ["T1", "C23"], ["T2"])
-    tt(T.TU[:], T.T2[:], T.BK[:], ALU.mult, ["T2", "BK"], ["TU"])
-    ts(T.R1[:], T.QX[:], 0.0, None, ALU.is_gt, None, ["QX"], ["R1"])
-    V(lambda v: v.memset(T.AT[:, 2048:NA], -1.0), w=["AT"])
-
-    def late_constants():
-        ts(T.DIAG[:], T.QX[:], c(2), None, ALU.is_equal, None, ["QX", "C0"], ["DIAG"])
-        ts(T.TRI[:], T.QX[:], c(2), None, ALU.is_gt, None, ["QX", "C0"], ["TRI"])
-        ts(T.NEWL[:], T.NEWL[:], c(7), None, ALU.mult, None, ["NEWL", "C7"], ["NEWL"])
-        ts(T.DWL[:], T.DWL[:], c(2), None, ALU.add, None, ["DWL", "C0"], ["DWL"])
-        ts(T.QW[:], T.QW[:], 127, None, ALU.bitwise_and, None, ["QW"], ["QW"])
-        ts(T.W3[:], T.QW[:], c(0), None, ALU.is_equal, None, ["QW", "C0"], ["W3"])
+    ts(T.ID[:], T.Q[:, 0:128], c(0), None, ALU.is_equal, None, ["Q", "C0"], ["ID"], 128)
+    ts(T.NI[:], T.Q[:, 0:128], c(0), -1.0, ALU.is_equal, ALU.mult, ["Q", "C0"], ["NI"], 128)
+    ts(T.ZD[:], T.Q[:], c(24), None, ALU.is_equal, None, ["Q", "C24"], ["ZD"], 144)
+    cp(T.SWF[:], T.SWB[:], ["SWB"], ["SWF"], 512)
+    ts(T.DW[:], T.Q[:, 0:128], c(0), c(11), ALU.is_equal, ALU.mult, ["Q", "C0", "C11"], ["DW"], 128)
+    ts(T.PN[:], T.Q[:, 0:128], c(0), 128.0, ALU.is_equal, ALU.mult, ["Q", "C0"], ["PN"], 128)
+    ts(T.BK[:], T.QG[:], c(1), None, ALU.is_equal, None, ["QG", "C0"], ["BK"], 128)
+    ts(T.T1[:], T.QX2[:], c(2), -16.0, ALU.is_lt, ALU.mult, ["QX2", "C0"], ["T1"], 128)
+    ts(T.T2[:], T.T1[:], 1.0, c(23), ALU.add, ALU.mult, ["T1", "C23"], ["T2"], 128)
+    tt(T.TU[:], T.T2[:], T.BK[:], ALU.mult, ["T2", "BK"], ["TU"], 256)
+    ts(T.R1[:], T.QX[:], 0.0, None, ALU.is_gt, None, ["QX"], ["R1"], 384)
+    ms(T.AT[:, 2048:NA], -1.0, ["AT"], 1152)
+    ts(T.DIAG[:], T.QX[:], c(2), None, ALU.is_equal, None, ["QX", "C0"], ["DIAG"], 384)
+    ts(T.TRI[:], T.QX[:], c(2), None, ALU.is_gt, None, ["QX", "C0"], ["TRI"], 384)
+    ts(T.NEWL[:], T.NEWL[:], c(7), None, ALU.mult, None, ["NEWL", "C7"], ["NEWL"], 384)
+    ts(T.DWL[:], T.DWL[:], c(2), None, ALU.add, None, ["DWL", "C0"], ["DWL"])
+    ts(T.QW[:], T.QW[:], 127, None, ALU.bitwise_and, None, ["QW"], ["QW"], 768)
+    ts(T.W3[:], T.QW[:], c(0), None, ALU.is_equal, None, ["QW", "C0"], ["W3"], 768)
 
     sl = lambda s: slice(12 * st[s], 12 * st[s] + 12)
     sw = lambda s: slice(192 * st[s], 192 * st[s] + 192)
@@ -240,23 +302,23 @@ def rank_program(g, core, T, topo):
 
     for s in "AB":
         vx_lists(s, lambda u: T.W0I[:, 12 * st[s] + u:12 * st[s] + 12:2], "W0I")
-    cp(T.AT[:, 0:2048], T.ATI[:], ["ATI"], ["AT"])
+    cp(T.AT[:, 0:2048], T.ATI[:], ["ATI"], ["AT"], 2048)
 
     def agather(s, key=True):
-        act(T.GA[:, sw(s)], T.AT[:].indirect(T.VL0[:, sl(s)]), ACT.Identity, 0.0, 1.0, ["AT", "VL" + s], ["GA" + s])
+        act(T.GA[:, sw(s)], T.AT[:].indirect(T.VL0[:, sl(s)]), ACT.Identity, 0.0, 1.0, ["AT", "VL" + s], ["GA" + s], 192 * GA_C)
         if key:
-            dma("Y", T.GA3[:, sl(s), :], T.GA[:, sw(s)], "dg" + s, ["GA" + s], ["G3" + s])
+            dma("Y", T.GA3[:, sl(s), :], T.GA[:, sw(s)], "dg" + s, ["GA" + s], ["G3" + s], 96)
 
     def xgather(s):
-        act(T.XV[:, sw(s)], T.XO[:].indirect(T.VX0[:, sl(s)]), ACT.Identity, 0.0, 1.0, XOALL + ["VX" + s], ["XV" + s])
+        act(T.XV[:, sw(s)], T.XO[:].indirect(T.VX0[:, sl(s)]), ACT.Identity, 0.0, 1.0, XOALL + ["VX" + s], ["XV" + s], 192 * GA_C)
 
-    def swap4(out, o0, mat, src, key, r, stop, n=1):
+    def swap4(out, o0, mat, src, key, r, stop, n=1, f=1):
         k = 0
         for rep in range(n):
             for u in range(2):
                 for v in range(2):
                     k += 1
-                    mm(out[:, o0 + v:o0 + 12:2, :], mat(v, u), src(u), False, stop and k == 4 * n, r, [key])
+                    mm(out[:, o0 + v:o0 + 12:2, :], mat(v, u), src(u), False, stop and k == 4 * n, r, [key], 96 * f)
 
     def xv(s):
         return lambda u: T.XV[:, 192 * st[s] + 96 * u:192 * st[s] + 96 * u + 96]
@@ -264,19 +326,19 @@ def rank_program(g, core, T, topo):
     def zswap(s, first):
         o = B("pZ", s)
         if first:
-            mm(o[:, 0:12, :], T.ZR[:], T.XV[:, sw(s)], True, False, ["ZR", "XV" + s], ["pZ" + s])
+            mm(o[:, 0:12, :], T.ZR[:], T.XV[:, sw(s)], True, False, ["ZR", "XV" + s], ["pZ" + s], 192)
         else:
-            mm(o[:, 0:12, :], T.ID[:], B("Z", s)[:, 0:192], True, False, ["ID", "Z" + s], ["pZ" + s])
+            mm(o[:, 0:12, :], T.ID[:], B("Z", s)[:, 0:192], True, False, ["ID", "Z" + s], ["pZ" + s], 192)
         swap4(o, 0, swb, xv(s), "pZ" + s, ["XV" + s, "SWB"], True, 2 if first else 1)
 
     def zact(s, first, final=False):
         bias = 127.75 if first else 63.75
         src = B("pZ", s)[:, 0:12, :]
         if final:
-            act(B("ZF", s)[:], src, ACT.Identity, bias, 0.5, ["pZ" + s], ["ZF" + s])
+            act(B("ZF", s)[:], src, ACT.Identity, bias, 0.5, ["pZ" + s], ["ZF" + s], 192)
         else:
             for d in range(2):
-                act(B("Z", s)[:, 192 * d:192 * d + 192], src, ACT.Identity, bias, 0.5, ["pZ" + s], ["Z" + s])
+                act(B("Z", s)[:, 192 * d:192 * d + 192], src, ACT.Identity, bias, 0.5, ["pZ" + s], ["Z" + s], 192)
 
     def lists(s, L):
         lt, cl = B("LT", s), B("CL", s)
@@ -284,64 +346,7 @@ def rank_program(g, core, T, topo):
             o = 192 * st[s] + 32 * b
             tr(lt[:, b:192:6], T.GA[:, o:o + 32], ["GA" + s], ["LT" + s])
         for g2 in range(2):
-            ts(cl[:, g2:12 * L:2], lt[:, 96 * g2:96 * g2 + 6 * L], 8.0 + H * g2, None, ALU.add, None, ["LT" + s], ["CL" + s])
-
-    def gakey(s):
-        o = B("pK", s)
-        mm(o[:, 0:12, :], T.ZR[:], B("Z", s)[:, 0:192], True, False, ["ZR", "Z" + s], ["pK" + s])
-        swap4(o, 0, swf, lambda u: T.GA3[:, 12 * st[s] + u:12 * st[s] + 12:2, :], "pK" + s, ["G3" + s, "SWF"], False)
-
-    def valid(s, t):
-        thr = 8 if t else 9
-        act(B("VAL", s)[:], B("pD", s)[:, 0:192], ACT.Sign, c(thr), -1.0, ["pD" + s, "C%d" % thr], ["VAL" + s])
-
-    def keymm(s):
-        mm(B("pK", s)[:, 0:12, :], T.DW[:], B("VAL", s)[:], False, True, ["DW", "VAL" + s], ["pK" + s])
-
-    def umm(s, k):
-        o = B("pZ", s)[:, 12:24, :]
-        mm(o, T.TU[:], B("VAL", s)[:], True, k == 0, ["TU", "VAL" + s], ["pZ" + s])
-        if k:
-            mm(o, T.ID[:], B("F", s)[:], False, True, ["ID", "F" + s], ["pZ" + s])
-
-    def frelu(s):
-        act(B("F", s)[:], B("pZ", s)[:, 12:24, :], ACT.Relu, c(10), 1.0, ["pZ" + s, "C10"], ["F" + s])
-
-    def decode(s, last):
-        kt, sc, vi, vj = B("KT", s), B("SC", s), B("VI", s), B("VJ", s)
-        tr(kt[:], B("pK", s)[:, 0:12, :], ["pK" + s], ["KT" + s])
-        V(lambda v: v.tensor_tensor_scan(sc[:], T.R1[:, 0:192], kt[:], 0.0, ALU.mult, ALU.max), ["R1", "KT" + s], ["SC" + s])
-        cp(vi[:], sc[:, 15:192:16], ["SC" + s], ["VI" + s])
-        ts(vj[:], vi[:], 4095, None, ALU.bitwise_and, None, ["VI" + s], ["VJ" + s])
-        cp(T.VL0[:, sl(s)], vj[:], ["VJ" + s], ["VL" + s])
-        vx_lists(s, lambda u: vj[:, u:12:2], "VJ" + s)
-        if last:
-            cp(T.VLF[:, sl(s)], vj[:], ["VJ" + s], ["VLF" + s])
-            ts(T.VXN[:, sl(s)], vj[:], 8.0, None, ALU.add, None, ["VJ" + s], ["VXN" + s])
-
-    def b_gather(s):
-        act(B("XG", s)[:], T.X2[:].indirect(B("CL", s)[:, 0:24]), ACT.Identity, 0.0, 1.0, X2ALL + ["CL" + s], ["XG" + s])
-
-    def b_sub(s):
-        o = B("pS", s)[:, 0:24, :]
-        mm(o, T.ID[:], B("XG", s)[:], True, False, ["ID", "XG" + s], ["pS" + s])
-        mm(o, T.NI[:], B("Z", s)[:], False, True, ["NI", "Z" + s], ["pS" + s])
-
-    def b_abs(s):
-        act(B("AB", s)[:, 0:384], B("pS", s)[:, 0:24, :], ACT.Abs, 128.0, 1.0, ["pS" + s], ["AB%s0" % s, "AB%s1" % s])
-
-    def vgather(s, i, n):
-        tt(B("CD", s)[:, 192 * i:192 * (i + n)], T.X2[:].indirect(B("CL", s)[:, 12 * i:12 * (i + n)]),
-           B("Z", s)[:, 0:192 * n], ALU.subtract, X2ALL + ["CL" + s, "Z" + s], ["CD%s%d" % (s, x) for x in range(i, i + n)])
-
-    def vabs(s, i, n):
-        act(B("AB", s)[:, 192 * i:192 * (i + n)], B("CD", s)[:, 192 * i:192 * (i + n)], ACT.Abs, 128.0, 1.0,
-            ["CD%s%d" % (s, x) for x in range(i, i + n)], ["AB%s%d" % (s, x) for x in range(i, i + n)])
-
-    def dist(s, i, n, L, start):
-        for x in range(i, i + n):
-            mm(B("pD", s)[:, 0:192], T.ZD[:, 15 - x:143 - x], B("AB", s)[:, 192 * x:192 * x + 192], start and x == i,
-               x == L - 1, ["ZD", "AB%s%d" % (s, x)], ["pD" + s])
+            ts(cl[:, g2:12 * L:2], lt[:, 96 * g2:96 * g2 + 6 * L], 8.0 + H * g2, None, ALU.add, None, ["LT" + s], ["CL" + s], 90)
 
     def begin(s, L):
         agather(s)
@@ -350,82 +355,82 @@ def rank_program(g, core, T, topo):
         zact(s, True)
         lists(s, L)
 
-    def period(sel, k, blk, kb, t):
+    def bulk(s, k, t):
+        L = 14 + t
+        pd, ab, cd, cl, z = B("pD", s), B("AB", s), B("CD", s), B("CL", s), B("Z", s)
+        for i in range(0, 2 * NB, 2):
+            act(B("XG", s)[:], T.X2[:].indirect(cl[:, 12 * i:12 * i + 24]), ACT.Identity, 0.0, 1.0, X2ALL + ["CL" + s], ["XG" + s], 384 * GA_C)
+            o = B("pS", s)[:, 0:24, :]
+            mm(o, T.ID[:], B("XG", s)[:], True, False, ["ID", "XG" + s], ["pS" + s], 384)
+            mm(o, T.NI[:], z[:], False, True, ["NI", "Z" + s], ["pS" + s], 384)
+            act(ab[:, 192 * i:192 * i + 384], o, ACT.Abs, 128.0, 1.0, ["pS" + s], ["AB%s%d" % (s, i), "AB%s%d" % (s, i + 1)], 384)
+        for i in range(2 * NB, L, 2):
+            n = min(2, L - i)
+            tt(cd[:, 192 * i:192 * (i + n)], T.X2[:].indirect(cl[:, 12 * i:12 * (i + n)]), z[:, 0:192 * n], ALU.subtract,
+               X2ALL + ["CL" + s, "Z" + s], ["CD%s%d" % (s, x) for x in range(i, i + n)], 192 * n * GA_C)
+        for i, n in ABS:
+            n = min(n, L - i)
+            act(ab[:, 192 * i:192 * (i + n)], cd[:, 192 * i:192 * (i + n)], ACT.Abs, 128.0, 1.0,
+                ["CD%s%d" % (s, x) for x in range(i, i + n)], ["AB%s%d" % (s, x) for x in range(i, i + n)], 192 * n)
+        if k:
+            mm(pd[:, 0:192], T.PN[:], B("F", s)[:], True, False, ["PN", "F" + s], ["pD" + s], 192)
+        todo = [x for i in ORDER for x in (i, i + 1)] + [14] * t
+        for j, x in enumerate(todo):
+            mm(pd[:, 0:192], T.ZD[:, 15 - x:143 - x], ab[:, 192 * x:192 * x + 192], j == 0 and not k, j == L - 1,
+               ["ZD", "AB%s%d" % (s, x)], ["pD" + s], 192)
+        o = B("pK", s)
+        mm(o[:, 0:12, :], T.ZR[:], z[:, 0:192], True, False, ["ZR", "Z" + s], ["pK" + s], 192)
+        swap4(o, 0, swf, lambda u: T.GA3[:, 12 * st[s] + u:12 * st[s] + 12:2, :], "pK" + s, ["G3" + s, "SWF"], False, 1, 4)
+
+    def select(s, k, t):
         L = 14 + t
         last = k == 3
-        if blk:
-            b_gather(blk)
-            vgather(blk, 2, 2)
-            vgather(blk, 4, 2)
-        if sel:
-            valid(sel, t)
-        if blk:
-            b_sub(blk)
-        if sel:
-            keymm(sel)
-            if not last:
-                umm(sel, k)
-        if blk:
-            b_abs(blk)
-        elif not t:
-            late_constants()
-        if sel:
-            decode(sel, last)
-        if blk:
-            vabs(blk, 2, 4)
-            if kb:
-                mm(B("pD", blk)[:, 0:192], T.PN[:], B("F", blk)[:], True, False, ["PN", "F" + blk], ["pD" + blk])
-            dist(blk, 0, 6, L, not kb)
-        if sel:
-            if not last:
-                frelu(sel)
-                agather(sel)
-            xgather(sel)
-        if blk:
-            vgather(blk, 6, 2)
-            vgather(blk, 8, 2)
-        if sel:
-            zswap(sel, False)
-            if last:
-                diff(sel)
-            zact(sel, False, last)
-            if not last:
-                lists(sel, L)
-            elif not t:
-                agather(sel, False)
-        if blk:
-            vabs(blk, 6, 4)
-            gakey(blk)
-            dist(blk, 6, 4, L, False)
-            vgather(blk, 10, 2)
-            vgather(blk, 12, 2)
-            if L == 15:
-                vgather(blk, 14, 1)
-        if sel and last:
-            votes(sel, t)
-        if blk:
-            vabs(blk, 10, L - 10)
-            dist(blk, 10, L - 10, L, False)
-
-    def diff(s):
-        o = B("pS", s)
-        mm(o[:, 0:12, :], T.NI[:], B("Z", s)[:, 0:192], True, False, ["NI", "Z" + s], ["pS" + s])
-        swap4(o, 0, swb, xv(s), "pS" + s, ["XV" + s, "SWB"], True)
+        thr = 8 if t else 9
+        kt, sc, vi, vj = B("KT", s), B("SC", s), B("VI", s), B("VJ", s)
+        act(B("VAL", s)[:], B("pD", s)[:, 0:192], ACT.Sign, c(thr), -1.0, ["pD" + s, "C%d" % thr], ["VAL" + s], 192)
+        mm(B("pK", s)[:, 0:12, :], T.DW[:], B("VAL", s)[:], False, True, ["DW", "VAL" + s], ["pK" + s], 192)
+        tr(kt[:], B("pK", s)[:, 0:12, :], ["pK" + s], ["KT" + s], 192)
+        V(lambda v: v.tensor_tensor_scan(sc[:], T.R1[:, 0:192], kt[:], 0.0, ALU.mult, ALU.max), ["R1", "KT" + s], ["SC" + s], 192)
+        cp(vi[:], sc[:, 15:192:16], ["SC" + s], ["VI" + s])
+        ts(vj[:], vi[:], 4095, None, ALU.bitwise_and, None, ["VI" + s], ["VJ" + s])
+        cp(T.VL0[:, sl(s)], vj[:], ["VJ" + s], ["VL" + s])
+        vx_lists(s, lambda u: vj[:, u:12:2], "VJ" + s)
+        if last:
+            cp(T.VLF[:, sl(s)], vj[:], ["VJ" + s], ["VLF" + s])
+            ts(T.VXN[:, sl(s)], vj[:], 8.0, None, ALU.add, None, ["VJ" + s], ["VXN" + s])
+        else:
+            o = B("pD", s)[:, 192:384]
+            mm(o, T.TU[:], B("VAL", s)[:], True, k == 0, ["TU", "VAL" + s], ["pD" + s], 192)
+            if k:
+                mm(o, T.ID[:], B("F", s)[:], False, True, ["ID", "F" + s], ["pD" + s], 192)
+            act(B("F", s)[:], o, ACT.Relu, c(10), 1.0, ["pD" + s, "C10"], ["F" + s], 192)
+        if not (last and t):
+            agather(s, not last)
+        xgather(s)
+        zswap(s, False)
+        if last:
+            o = B("pS", s)
+            mm(o[:, 0:12, :], T.NI[:], B("Z", s)[:, 0:192], True, False, ["NI", "Z" + s], ["pS" + s], 192)
+            swap4(o, 0, swb, xv(s), "pS" + s, ["XV" + s, "SWB"], True)
+        zact(s, False, last)
+        if not last:
+            lists(s, L)
 
     def votes(s, t):
-        ts(B("GT", s)[:], B("pS", s)[:, 0:12, :], -128.0, None, ALU.is_gt, None, ["pS" + s], ["GT" + s])
+        ts(B("GT", s)[:], B("pS", s)[:, 0:12, :], -128.0, None, ALU.is_gt, None, ["pS" + s], ["GT" + s], 192)
+        mm(B("pK", s)[:, 0:12, :], T.BK[:], B("GT", s)[:], True, True, ["BK", "GT" + s], ["pK" + s], 192)
         o = B("pZ", s)
-        mm(o[:, 12:24, :], T.ZR[:], B("ZF", s)[:], True, False, ["ZR", "ZF" + s], ["pZ" + s])
+        mm(o[:, 12:24, :], T.ZR[:], B("ZF", s)[:], True, False, ["ZR", "ZF" + s], ["pZ" + s], 192)
         swap4(o, 12, swb, lambda u: B("ZF", s)[:, u:12:2, :], "pZ" + s, ["ZF" + s, "SWB"], True)
-        mm(B("pK", s)[:, 0:12, :], T.BK[:], B("GT", s)[:], True, True, ["BK", "GT" + s], ["pK" + s])
         zn = "ZN%d" % t
-        act(T[zn][:, sw(s)], o[:, 12:24, :], ACT.Identity, 0.0, 1.0, ["pZ" + s], [zn + s])
-        act(T.VF[:, sw(s)], T.IDT[:].indirect(T.VL0[:, sl(s)]), ACT.Identity, 0.0, 1.0, ["IDT", "VL" + s], ["VF" + s])
-        tr(B("KT", s)[:], B("pK", s)[:, 0:12, :], ["pK" + s], ["KT" + s])
+        act(T[zn][:, sw(s)], o[:, 12:24, :], ACT.Identity, 0.0, 1.0, ["pZ" + s], [zn + s], 192)
+        act(T.VF[:, sw(s)], T.IDT[:].indirect(T.VL0[:, sl(s)]), ACT.Identity, 0.0, 1.0, ["IDT", "VL" + s], ["VF" + s], 192 * GA_C)
+        tr(B("KT", s)[:], B("pK", s)[:, 0:12, :], ["pK" + s], ["KT" + s], 192)
         ts(T.WT[:, sl(s)], B("KT", s)[:, 0:192:16], 9.0, EPS, ALU.is_lt, ALU.add, ["KT" + s], ["WT" + s])
         for d in range(2):
-            cp(T.VB[:, 24 * d + 12 * st[s]:24 * d + 12 * st[s] + 12, :], T.VF[:, sw(s)], ["VF" + s], ["VB" + s])
-        wait_for("G", [zn + s], [])
+            cp(T.VB[:, 24 * d + 12 * st[s]:24 * d + 12 * st[s] + 12, :], T.VF[:, sw(s)], ["VF" + s], ["VB" + s], 192)
+        if s == "A":
+            cp(T.VB[:, 48:49, :], T.VF[:, 0:16], ["VFA"], ["VBA"])
         trs = []
         for q in range(4 * st[s], 4 * st[s] + 4):
             if q == rank:
@@ -436,45 +441,44 @@ def rank_program(g, core, T, topo):
             mask = sum(1 << e for e in topo.engines(core, dst)[j:j + 2])
             trs.append(RemoteDMATransfer(dst_ids=[DstId(rid=rid, pnc=pid)], dma_engine_mask=mask, remote_sem=T.sem["arr%d" % t],
                                          src=T[zn][:, 48 * q:48 * q + 48], dst=T["RZ%d" % t][:, 48 * rank:48 * rank + 48]))
-        g.remote_dma_fused(trs, local_sem=T.sem.lsem)
+        op("G", lambda q: q.remote_dma_fused(trs, local_sem=T.sem.lsem), [zn + s], [], 1.0, "lsem")
 
     def flips(t):
-        all_, ear = T.pKA, T.pKB
-        act(T.XW[:], T.XO[:].indirect(T.VXN[:]), ACT.Identity, 0.0, 1.0, XOALL + ["VXNA", "VXNB"], ["XW"])
-        mm(ear[:, 0:24, :], T.ZR[:], T["ZN%d" % t][:], True, False, ["ZR", "ZN%dA" % t, "ZN%dB" % t], ["pKB"])
+        rest, ear, gas, zn = T.pKA, T.pKB, ["GAA", "GAB"], "ZN%d" % t
+        act(T.XW[:], T.XO[:].indirect(T.VXN[:]), ACT.Identity, 0.0, 1.0, XOALL + ["VXNA", "VXNB"], ["XW"], 384 * GA_C)
+        for o, k in ((ear, "pKB"), (rest, "pKA")):
+            mm(o[:, 0:24, :], T.ZR[:], T[zn][:], True, False, ["ZR", zn + "A", zn + "B"], [k], 384)
         for b in range(24):
             e0 = 24 * b
-            ts(T.E[:, e0:e0 + 24, :], T.VB[:, b:b + 24, :], T.VLF[:, b:b + 1], T.WT[:, b:b + 1], ALU.is_equal, ALU.mult,
-               ["VBA", "VBB", "VLFA", "VLFB", "WTA", "WTB"], ["E%d" % b])
-            mm(all_[:, b:24, :], T.BK[:], T.E[:, e0:e0 + 24 - b, :], b == 0, False, ["BK", "E%d" % b], ["pKA"])
-            if b:
-                mm(all_[:, 0:b, :], T.BK[:], T.E[:, e0 + 24 - b:e0 + 24, :], False, b == 23, ["BK", "E%d" % b], ["pKA"])
+            ts(T.E[:, e0:e0 + 24, :], T.VB[:, b + 1:b + 25, :], T.VLF[:, b:b + 1], T.WT[:, b:b + 1], ALU.is_equal, ALU.mult,
+               ["VBA", "VBB", "VLFA", "VLFB", "WTA", "WTB"], ["E%d" % b], 192)
             if b < 23:
-                mm(ear[:, b + 1:24, :], T.BK[:], T.E[:, e0 + 1:e0 + 24 - b, :], False, False, ["BK", "E%d" % b], ["pKB"])
-        tt(T.DG[:], T.E[:, 0:576:24, :], T.TRI[:], ALU.mult, ["E%d" % b for b in range(24)] + ["TRI"], ["DG"])
-        mm(ear[:, 0:24, :], T.BK[:], T.DG[:], False, True, ["BK", "DG"], ["pKB"])
-        ts(T.DX[:], T.XW[:], c(12), c(13), ALU.mult, ALU.add, ["XW", "C12", "C13"], ["DX"])
-        ts(T.FL[:], all_[:, 0:24, :], 1.0, None, ALU.is_lt, None, ["pKA"], ["FL"])
+                mm(ear[:, b + 1:24, :], T.BK[:], T.E[:, e0:e0 + 23 - b, :], False, False, ["BK", "E%d" % b], ["pKB"], 368 - 16 * b)
+            mm(rest[:, 0:b + 1, :], T.BK[:], T.E[:, e0 + 23 - b:e0 + 24, :], False, b == 23, ["BK", "E%d" % b], ["pKA"], 16 + 16 * b)
+        tt(T.DG[:], T.E[:, 23:576:24, :], T.TRI[:], ALU.mult, ["E%d" % b for b in range(24)] + ["TRI"], ["DG"], 768)
+        act(T.RS[:], rest[:, 0:24, :], ACT.Identity, 0.0, 1.0, ["pKA"], ["RS"], 384)
+        mm(ear[:, 0:24, :], T.BK[:], T.DG[:], False, True, ["BK", "DG"], ["pKB"], 384)
+        ts(T.DX[:], T.XW[:], c(12), c(13), ALU.mult, ALU.add, ["XW", "C12", "C13"], ["DX"], 192)
         tt(T.S3[:], T.DWL[:], T.VLF[:], ALU.subtract, ["DWL", "VLFA", "VLFB"], ["S3"])
-        tt(T.DM[:], ear[:, 0:24, :], T.DIAG[:], ALU.mult, ["pKB", "DIAG"], ["DM"])
-        tt(T.FX[:], T.FL[:], T.DX[:], ALU.mult, ["FL", "DX"], ["FX"])
-        V(lambda v: v.tensor_tensor_scan(T.SC2[:], T.R1[:], T.DM[:], 0.0, ALU.mult, ALU.add), ["R1", "DM"], ["SC2"])
+        tt(T.DM[:], ear[:, 0:24, :], T.DIAG[:], ALU.mult, ["pKB", "DIAG"], ["DM"], 384)
+        tt(T.RT[:], ear[:, 0:24, :], T.RS[:], ALU.add, ["pKB", "RS"], ["RT"], 384)
+        V(lambda v: v.tensor_tensor_scan(T.SC2[:], T.R1[:], T.DM[:], 0.0, ALU.mult, ALU.add), ["R1", "DM"], ["SC2"], 384)
+        ts(T.FL[:], T.RT[:], 1.0, None, ALU.is_lt, None, ["RT"], ["FL"], 384)
         ts(T.S1[:], T.SC2[:, 15:384:16], 0.0, None, ALU.is_gt, None, ["SC2"], ["S1"])
         tt(T.S2[:], T.S1[:], T.S3[:], ALU.mult, ["S1", "S3"], ["S2"])
+        tt(T.FX[:], T.FL[:], T.DX[:], ALU.mult, ["FL", "DX"], ["FX"], 768)
         tt(T.S4[:], T.S2[:], T.VLF[:], ALU.add, ["S2", "VLFA", "VLFB"], ["S4"])
         ts(T.XOFF[:], T.S4[:], 8.0, None, ALU.add, None, ["S4"], ["XOFF"])
-        ga = ["GAA", "GAB"]
+        tt(T.XO[:].indirect(T.XOFF[:]), T.XW[:], T.FX[:], ALU.add, ["XW", "FX", "XOFF"], XOALL, 384 * SC_C)
         if not t:
+            both("dd", T.XO[:, 8:2056], ["XOb"])
             cp(T.AOFF[:], T.S4[:], ["S4"], ["AOFF"])
-            ts(T.AT[:, 2048:2432], T.GA[:], c(6), c(14), ALU.mult, ALU.add, ga + ["C6", "C14"], ["AT"])
-        tt(T.XO[:].indirect(T.XOFF[:]), T.XW[:], T.FX[:], ALU.add, ["XW", "FX", "XOFF"], XOALL)
-        if not t:
-            tt(T.AT[:].indirect(T.AOFF[:]), T.GA[:], T.NEWL[:], ALU.add, ga + ["NEWL", "AOFF", "AT"], ["AT"])
-            both("dd", T.XO[:, 8:2056], XOALL)
+            ts(T.AT[:, 2048:2432], T.GA[:], c(6), c(14), ALU.mult, ALU.add, gas + ["C6", "C14"], ["AT"], 384)
+            tt(T.AT[:].indirect(T.AOFF[:]), T.GA[:], T.NEWL[:], ALU.add, gas + ["NEWL", "AOFF", "AT"], ["AT"], 384 * SC_C)
 
     def arrivals(t):
         rz, zn = "RZ%d" % t, "ZN%d" % t
-        arrive("arr%d" % t, 14, rz)
+        op("R", None, [zn + "A", zn + "B"], [rz], 8.0, "arr%d" % t)
         for ph, pk in ((0, "pSA"), (1, "pSB"), (2, "pZB"))[2 * t:]:
             for r in range(8):
                 d = (rank - r) % 8
@@ -484,27 +488,25 @@ def rank_program(g, core, T, topo):
                     e = (ph - d) % 2
                     o = 256 * e + 32 * ((((ph - d) % 8 - e) // 2) % 4)
                 src, keys = (T[zn], [zn + "A", zn + "B"]) if r == rank else (T[rz], [rz])
-                mm(T[pk][:, 3 * r:3 * r + 3, :], T.W3[:, o:o + 128], src[:, 48 * r:48 * r + 48], True, True, ["W3"] + keys, [pk])
+                mm(T[pk][:, 3 * r:3 * r + 3, :], T.W3[:, o:o + 128], src[:, 48 * r:48 * r + 48], True, True, ["W3"] + keys, [pk], 64)
             n = 8 + 2048 + 384 * t
             if ph == 2:
-                act(T.XO[:, n:n + 384], T[pk][:, 0:24, :], ACT.Identity, -128.0, 1.0, [pk], ["XOn"])
+                act(T.XO[:, n:n + 384], T[pk][:, 0:24, :], ACT.Identity, -128.0, 1.0, [pk], ["XOn"], 384)
             else:
-                act(T.X2[:, ph * H + n:ph * H + n + 384], T[pk][:, 0:24, :], ACT.Identity, -128.0, 1.0, [pk], ["X2n"])
+                act(T.X2[:, ph * H + n:ph * H + n + 384], T[pk][:, 0:24, :], ACT.Identity, -128.0, 1.0, [pk], ["X2n"], 384)
 
     for t in range(2):
-        L = 14 + t
-        begin("A", L)
-        begin("B", L)
-        if t:
-            arrivals(0)
-        period(None, -1, "A", 0, t)
+        for s in "AB":
+            begin(s, 14 + t)
         for k in range(4):
-            period("A", k, "B", k, t)
-            period("B", k, "A" if k < 3 else None, k + 1, t)
+            for s in "AB":
+                bulk(s, k, t)
+                select(s, k, t)
+        for s in "AB":
+            votes(s, t)
         if t:
-            dma("Y", T.yv[:, :], T.VF[0:128:16, :], "dv", r=["VFA", "VFB"])
+            dma("Y", T.yv[:, :], T.VF[0:128:16, :], "dv", ["VFA", "VFB"], [], 12)
         flips(t)
-    arrivals(1)
-    dma("Y", T.yx[:, :], T.XO[:, 8:2824], "do", r=XOALL)
-    finish()
-    g.wait_ge(T.sem.lsem, 28)
+        arrivals(t)
+    dma("Y", T.yx[:, :], T.XO[:, 8:2824], "do", XOALL, [], 720)
+    emit(g, T, schedule(ops))

@@ -9,8 +9,10 @@ EPS = 2.0 ** -9
 NB = 1
 ABS = ((2, 2), (4, 2), (6, 4), (10, 2), (12, 3))
 ORDER = (2, 4, 0, 6, 8, 10, 12)
-CY, FV, FS, FP, PE, WAKE = 0.83e-3, 0.06, 0.07, 0.04, 0.45e-3, 0.08
+CY, FV, FS, FP, PE, WAKE = 0.83e-3, 0.06, 0.10, 0.04, 0.45e-3, 0.08
 GA_C, SC_C = 1.5, 3.5
+AHEAD = 2.2
+LOADS = {"dw": 4e3, "dl": 3e3, "dx": 2e3, "dy": 1e3}
 
 SCRATCH = {}
 
@@ -20,8 +22,8 @@ def _decl(dtype, where="sbuf", **shapes):
         SCRATCH[n] = (where, [128] + sh, dtype)
 
 
-_decl("bfloat16", X2=[2 * H], XO=[8 + NA], W3=[768], ZD=[144], BK=[128], ID=[128], NI=[128], PN=[128], DW=[128], TU=[128],
-      ZR=[128], SWB=[512], R1=[384], DIAG=[24, 16], TRI=[24, 16], E=[576, 16], DG=[24, 16], DX=[384], FX=[384], FL=[384],
+_decl("bfloat16", X2=[2 * H], XO=[8 + NA], XM=[384], W3=[768], ZD=[144], BK=[128], ID=[128], NI=[128], PN=[128], DW=[128],
+      TU=[128], ZR=[128], SWB=[512], R1=[384], DIAG=[24, 16], TRI=[24, 16], E=[576, 16], DG=[24, 16], DX=[384], FX=[384],
       XV=[384], XW=[384], ZN0=[384], ZN1=[384], RZ0=[384], RZ1=[384])
 _decl("float32", AT=[NA], IDT=[2816], C=[32], Q=[144], QX=[24, 16], QX2=[128], QG=[128], T1=[128], T2=[128], SWF=[512],
       NEWL=[384], DWL=[24], VLF=[24], WT=[24], VF=[384], DM=[384], SC2=[384], RS=[24, 16], RT=[384], S1=[24], S2=[24], S3=[24],
@@ -74,8 +76,8 @@ def schedule(ops):
     dmaq = 0.0
     while ready:
         st = [max(base[j], free.get(ops[j]["e"], 0.0)) for j in ready]
-        t0 = min(st) + 0.02
-        j = max((bl[x], -x, x) for x, s in zip(ready, st) if s <= t0)[2]
+        t0 = min(st) + 0.03
+        j = max((bl[x] + ops[x]["first"], -x, x) for x, s in zip(ready, st) if s <= t0)[2]
         ready.remove(j)
         o = ops[j]
         s = max(base[j], free.get(o["e"], 0.0))
@@ -167,9 +169,11 @@ def rank_program(g, core, T, topo):
     if rank is None:
         return
     ops = []
+    ahead = [0.0]
 
     def op(e, fn, r, w, c, sem=None, lat=0.0, by=0.0):
-        ops.append({"e": e, "fn": fn, "r": list(r), "w": list(w), "c": c, "sem": sem, "lat": lat, "by": by})
+        ops.append({"e": e, "fn": fn, "r": list(r), "w": list(w), "c": c, "sem": sem, "lat": lat, "by": by,
+                    "first": ahead[0] + LOADS.get(sem, 0.0)})
 
     def V(fn, r, w, n):
         op("V", fn, r, w, FV + max(64, n) * CY)
@@ -283,7 +287,7 @@ def rank_program(g, core, T, topo):
     ts(T.T2[:], T.T1[:], 1.0, c(23), ALU.add, ALU.mult, ["T1", "C23"], ["T2"], 128)
     tt(T.TU[:], T.T2[:], T.BK[:], ALU.mult, ["T2", "BK"], ["TU"], 256)
     ts(T.R1[:], T.QX[:], 0.0, None, ALU.is_gt, None, ["QX"], ["R1"], 384)
-    ms(T.AT[:, 2048:NA], -1.0, ["AT"], 1152)
+    ms(T.AT[:, 2048:NA], -1.0, ["ATn"], 1152)
     ts(T.DIAG[:], T.QX[:], c(2), None, ALU.is_equal, None, ["QX", "C0"], ["DIAG"], 384)
     ts(T.TRI[:], T.QX[:], c(2), None, ALU.is_gt, None, ["QX", "C0"], ["TRI"], 384)
     ts(T.NEWL[:], T.NEWL[:], c(7), None, ALU.mult, None, ["NEWL", "C7"], ["NEWL"], 384)
@@ -305,7 +309,7 @@ def rank_program(g, core, T, topo):
     cp(T.AT[:, 0:2048], T.ATI[:], ["ATI"], ["AT"], 2048)
 
     def agather(s, key=True):
-        act(T.GA[:, sw(s)], T.AT[:].indirect(T.VL0[:, sl(s)]), ACT.Identity, 0.0, 1.0, ["AT", "VL" + s], ["GA" + s], 192 * GA_C)
+        act(T.GA[:, sw(s)], T.AT[:].indirect(T.VL0[:, sl(s)]), ACT.Identity, 0.0, 1.0, ["AT", "ATn", "VL" + s], ["GA" + s], 192 * GA_C)
         if key:
             dma("Y", T.GA3[:, sl(s), :], T.GA[:, sw(s)], "dg" + s, ["GA" + s], ["G3" + s], 96)
 
@@ -417,7 +421,7 @@ def rank_program(g, core, T, topo):
             lists(s, L)
 
     def votes(s, t):
-        ts(B("GT", s)[:], B("pS", s)[:, 0:12, :], -128.0, None, ALU.is_gt, None, ["pS" + s], ["GT" + s], 192)
+        act(B("GT", s)[:], B("pS", s)[:, 0:12, :], ACT.Sign, 127.5, 1.0, ["pS" + s], ["GT" + s], 192)
         mm(B("pK", s)[:, 0:12, :], T.BK[:], B("GT", s)[:], True, True, ["BK", "GT" + s], ["pK" + s], 192)
         o = B("pZ", s)
         mm(o[:, 12:24, :], T.ZR[:], B("ZF", s)[:], True, False, ["ZR", "ZF" + s], ["pZ" + s], 192)
@@ -426,7 +430,7 @@ def rank_program(g, core, T, topo):
         act(T[zn][:, sw(s)], o[:, 12:24, :], ACT.Identity, 0.0, 1.0, ["pZ" + s], [zn + s], 192)
         act(T.VF[:, sw(s)], T.IDT[:].indirect(T.VL0[:, sl(s)]), ACT.Identity, 0.0, 1.0, ["IDT", "VL" + s], ["VF" + s], 192 * GA_C)
         tr(B("KT", s)[:], B("pK", s)[:, 0:12, :], ["pK" + s], ["KT" + s], 192)
-        ts(T.WT[:, sl(s)], B("KT", s)[:, 0:192:16], 9.0, EPS, ALU.is_lt, ALU.add, ["KT" + s], ["WT" + s])
+        ts(T.WT[:, sl(s)], B("KT", s)[:, 0:192:16], 1.0, EPS, ALU.is_lt, ALU.add, ["KT" + s], ["WT" + s])
         for d in range(2):
             cp(T.VB[:, 24 * d + 12 * st[s]:24 * d + 12 * st[s] + 12, :], T.VF[:, sw(s)], ["VF" + s], ["VB" + s], 192)
         if s == "A":
@@ -446,35 +450,36 @@ def rank_program(g, core, T, topo):
     def flips(t):
         rest, ear, gas, zn = T.pKA, T.pKB, ["GAA", "GAB"], "ZN%d" % t
         act(T.XW[:], T.XO[:].indirect(T.VXN[:]), ACT.Identity, 0.0, 1.0, XOALL + ["VXNA", "VXNB"], ["XW"], 384 * GA_C)
-        for o, k in ((ear, "pKB"), (rest, "pKA")):
-            mm(o[:, 0:24, :], T.ZR[:], T[zn][:], True, False, ["ZR", zn + "A", zn + "B"], [k], 384)
-        for b in range(24):
+        act(T.DX[:], T.XW[:], ACT.Identity, c(13), c(12), ["XW", "C12", "C13"], ["DX"], 384)
+        mm(ear[:, 0:24, :], T.ZR[:], T[zn][:], True, False, ["ZR", zn + "A", zn + "B"], ["pKB"], 384)
+        for b in range(23, -1, -1):
             e0 = 24 * b
             ts(T.E[:, e0:e0 + 24, :], T.VB[:, b + 1:b + 25, :], T.VLF[:, b:b + 1], T.WT[:, b:b + 1], ALU.is_equal, ALU.mult,
                ["VBA", "VBB", "VLFA", "VLFB", "WTA", "WTB"], ["E%d" % b], 192)
             if b < 23:
                 mm(ear[:, b + 1:24, :], T.BK[:], T.E[:, e0:e0 + 23 - b, :], False, False, ["BK", "E%d" % b], ["pKB"], 368 - 16 * b)
-            mm(rest[:, 0:b + 1, :], T.BK[:], T.E[:, e0 + 23 - b:e0 + 24, :], False, b == 23, ["BK", "E%d" % b], ["pKA"], 16 + 16 * b)
-        tt(T.DG[:], T.E[:, 23:576:24, :], T.TRI[:], ALU.mult, ["E%d" % b for b in range(24)] + ["TRI"], ["DG"], 768)
+            mm(rest[:, 0:b + 1, :], T.BK[:], T.E[:, e0 + 23 - b:e0 + 24, :], b == 23, b == 0, ["BK", "E%d" % b], ["pKA"], 16 + 16 * b)
+        for h in (18, 12, 6, 0):
+            tt(T.DG[:, h:h + 6, :], T.E[:, 24 * h + 23:24 * h + 144:24, :], T.TRI[:, h:h + 6, :], ALU.mult,
+               ["E%d" % b for b in range(h, h + 6)] + ["TRI"], ["DG"], 192)
         act(T.RS[:], rest[:, 0:24, :], ACT.Identity, 0.0, 1.0, ["pKA"], ["RS"], 384)
         mm(ear[:, 0:24, :], T.BK[:], T.DG[:], False, True, ["BK", "DG"], ["pKB"], 384)
-        ts(T.DX[:], T.XW[:], c(12), c(13), ALU.mult, ALU.add, ["XW", "C12", "C13"], ["DX"], 192)
         tt(T.S3[:], T.DWL[:], T.VLF[:], ALU.subtract, ["DWL", "VLFA", "VLFB"], ["S3"])
         tt(T.DM[:], ear[:, 0:24, :], T.DIAG[:], ALU.mult, ["pKB", "DIAG"], ["DM"], 384)
         tt(T.RT[:], ear[:, 0:24, :], T.RS[:], ALU.add, ["pKB", "RS"], ["RT"], 384)
         V(lambda v: v.tensor_tensor_scan(T.SC2[:], T.R1[:], T.DM[:], 0.0, ALU.mult, ALU.add), ["R1", "DM"], ["SC2"], 384)
-        ts(T.FL[:], T.RT[:], 1.0, None, ALU.is_lt, None, ["RT"], ["FL"], 384)
+        ts(T.pZA[:, 0:24, :], T.RT[:], 1.0, None, ALU.is_lt, None, ["RT"], ["pZA"], 384)
         ts(T.S1[:], T.SC2[:, 15:384:16], 0.0, None, ALU.is_gt, None, ["SC2"], ["S1"])
         tt(T.S2[:], T.S1[:], T.S3[:], ALU.mult, ["S1", "S3"], ["S2"])
-        tt(T.FX[:], T.FL[:], T.DX[:], ALU.mult, ["FL", "DX"], ["FX"], 768)
+        tt(T.FX[:], T.pZA[:, 0:24, :], T.DX[:], ALU.mult, ["pZA", "DX"], ["FX"], 384)
         tt(T.S4[:], T.S2[:], T.VLF[:], ALU.add, ["S2", "VLFA", "VLFB"], ["S4"])
         ts(T.XOFF[:], T.S4[:], 8.0, None, ALU.add, None, ["S4"], ["XOFF"])
         tt(T.XO[:].indirect(T.XOFF[:]), T.XW[:], T.FX[:], ALU.add, ["XW", "FX", "XOFF"], XOALL, 384 * SC_C)
         if not t:
             both("dd", T.XO[:, 8:2056], ["XOb"])
             cp(T.AOFF[:], T.S4[:], ["S4"], ["AOFF"])
-            ts(T.AT[:, 2048:2432], T.GA[:], c(6), c(14), ALU.mult, ALU.add, gas + ["C6", "C14"], ["AT"], 384)
-            tt(T.AT[:].indirect(T.AOFF[:]), T.GA[:], T.NEWL[:], ALU.add, gas + ["NEWL", "AOFF", "AT"], ["AT"], 384 * SC_C)
+            act(T.AT[:, 2048:2432], T.GA[:], ACT.Identity, c(14), c(6), gas + ["C6", "C14"], ["ATn"], 384)
+            tt(T.AT[:].indirect(T.AOFF[:]), T.GA[:], T.NEWL[:], ALU.add, gas + ["NEWL", "AOFF"], ["AT", "ATn"], 384 * SC_C)
 
     def arrivals(t):
         rz, zn = "RZ%d" % t, "ZN%d" % t
@@ -489,24 +494,32 @@ def rank_program(g, core, T, topo):
                     o = 256 * e + 32 * ((((ph - d) % 8 - e) // 2) % 4)
                 src, keys = (T[zn], [zn + "A", zn + "B"]) if r == rank else (T[rz], [rz])
                 mm(T[pk][:, 3 * r:3 * r + 3, :], T.W3[:, o:o + 128], src[:, 48 * r:48 * r + 48], True, True, ["W3"] + keys, [pk], 64)
-            n = 8 + 2048 + 384 * t
-            if ph == 2:
-                act(T.XO[:, n:n + 384], T[pk][:, 0:24, :], ACT.Identity, -128.0, 1.0, [pk], ["XOn"], 384)
+            n = 8 + 2048
+            if t:
+                out, key = T.XM[:], "XM"
+            elif ph == 2:
+                out, key = T.XO[:, n:n + 384], "XOn"
             else:
-                act(T.X2[:, ph * H + n:ph * H + n + 384], T[pk][:, 0:24, :], ACT.Identity, -128.0, 1.0, [pk], ["X2n"], 384)
+                out, key = T.X2[:, ph * H + n:ph * H + n + 384], "X2n"
+            act(out, T[pk][:, 0:24, :], ACT.Identity, -128.0, 1.0, [pk], [key], 384)
 
     for t in range(2):
         for s in "AB":
             begin(s, 14 + t)
         for k in range(4):
             for s in "AB":
+                ahead[0] = AHEAD if s == "A" else 0.0
                 bulk(s, k, t)
                 select(s, k, t)
+        ahead[0] = 0.0
         for s in "AB":
             votes(s, t)
         if t:
             dma("Y", T.yv[:, :], T.VF[0:128:16, :], "dv", ["VFA", "VFB"], [], 12)
+            arrivals(t)
         flips(t)
-        arrivals(t)
-    dma("Y", T.yx[:, :], T.XO[:, 8:2824], "do", XOALL, [], 720)
+        if not t:
+            arrivals(t)
+    dma("Y", T.yx[:, 2432:2816], T.XM[:], "dv", ["XM"], [], 96)
+    dma("Y", T.yx[:, 0:2432], T.XO[:, 8:2440], "do", XOALL, [], 620)
     emit(g, T, schedule(ops))

from concourse.bass import DstId, RemoteDMATransfer
from concourse.mybir import AluOpType, ActivationFunctionType

ALU = AluOpType
ACT = ActivationFunctionType
H = 8 + 2816
NA = 2816 + 384
EPS = 2.0 ** -9
NB = 1
ABS = ((2, 2), (4, 2), (6, 4), (10, 2), (12, 3))
ORDER = (2, 4, 0, 6, 8, 10, 12)
CY, FV, FS, FP, PE, WAKE = 0.83e-3, 0.06, 0.10, 0.04, 0.45e-3, 0.08
GA_C, SC_C = 1.5, 3.5
AHEAD = 2.2
LOADS = {"dw": 4e3, "dl": 3e3, "dx": 2e3, "dy": 1e3}

SCRATCH = {}


def _decl(dtype, where="sbuf", **shapes):
    for n, sh in shapes.items():
        SCRATCH[n] = (where, [128] + sh, dtype)


_decl("bfloat16", X2=[2 * H], XO=[8 + NA], XM=[384], W3=[768], ZD=[144], BK=[128], ID=[128], NI=[128], PN=[128], DW=[128],
      TU=[128], ZR=[128], SWB=[512], R1=[384], DIAG=[24, 16], TRI=[24, 16], E=[576, 16], DG=[24, 16], DX=[384], FX=[384],
      XV=[384], XW=[384], ZN0=[384], ZN1=[384], RZ0=[384], RZ1=[384])
_decl("float32", AT=[NA], IDT=[2816], C=[32], Q=[144], QX=[24, 16], QX2=[128], QG=[128], T1=[128], T2=[128], SWF=[512],
      NEWL=[384], DWL=[24], VLF=[24], WT=[24], VF=[384], DM=[384], SC2=[384], RS=[24, 16], RT=[384], S1=[24], S2=[24], S3=[24],
      S4=[24], GA=[384], GA3=[24, 16])
_decl("int32", ATI=[2048], W0I=[24], PI=[8], QW=[768])
_decl("uint16", VL0=[24], VX0=[24], VXN=[24], VB=[49, 16], AOFF=[24], XOFF=[24])
for _s in "AB":
    _decl("bfloat16", **{"CD" + _s: [3072], "AB" + _s: [3072], "XG" + _s: [384], "Z" + _s: [384], "ZF" + _s: [12, 16],
                         "VAL" + _s: [192], "F" + _s: [192], "GT" + _s: [192]})
    _decl("float32", **{"LT" + _s: [192], "KT" + _s: [192], "SC" + _s: [192]})
    _decl("int32", **{"VI" + _s: [12], "VJ" + _s: [12]})
    _decl("uint16", **{"CL" + _s: [192]})
    _decl("float32", "psum", **{"pD" + _s: [512], "pK" + _s: [32, 16], "pZ" + _s: [32, 16], "pS" + _s: [32, 16]})
SEMAPHORES = ["sv", "ss", "sp", "sg", "dw", "dl", "dx", "dy", "dd", "do", "dv", "dgA", "dgB", "arr0", "arr1", "lsem"]


def schedule(ops):
    preds, lastw, readers = [], {}, {}
    for j, o in enumerate(ops):
        p = {}
        for k in o["r"]:
            if k in lastw:
                p[lastw[k]] = 0 if k[0] == "p" and ops[lastw[k]]["e"] == o["e"] else 1
            if k[0] == "p":
                for x in readers.get(k, ()):
                    p.setdefault(x, 0 if ops[x]["e"] == o["e"] else 1)
        for k in o["w"]:
            for x in ([lastw[k]] if k in lastw else []) + readers.get(k, []):
                same = ops[x]["e"] == o["e"] or (o["sem"] and ops[x]["sem"] == o["sem"])
                p.setdefault(x, 0 if same else 1)
        p.pop(j, None)
        preds.append(p)
        for k in o["r"]:
            readers.setdefault(k, []).append(j)
        for k in o["w"]:
            lastw[k] = j
            readers[k] = []
    n = len(ops)
    succ = [[] for _ in range(n)]
    for j in range(n):
        for i in preds[j]:
            succ[i].append(j)
    bl = [0.0] * n
    for j in range(n - 1, -1, -1):
        bl[j] = ops[j]["c"] + ops[j]["lat"] + max([bl[x] + WAKE for x in succ[j]] or [0.0])
    left = [len(preds[j]) for j in range(n)]
    base = [0.0] * n
    free, out = {}, []
    ready = [j for j in range(n) if not left[j]]
    dmaq = 0.0
    while ready:
        st = [max(base[j], free.get(ops[j]["e"], 0.0)) for j in ready]
        t0 = min(st) + 0.03
        j = max((bl[x] + ops[x]["first"], -x, x) for x, s in zip(ready, st) if s <= t0)[2]
        ready.remove(j)
        o = ops[j]
        s = max(base[j], free.get(o["e"], 0.0))
        fin = free[o["e"]] = s + o["c"]
        if o["lat"]:
            dmaq = max(dmaq, fin) + o["by"]
            fin = max(dmaq, fin) + o["lat"]
        out.append(o)
        for x in succ[j]:
            base[x] = max(base[x], fin + WAKE if preds[x][j] else s + o["c"])
            left[x] -= 1
            if not left[x]:
                ready.append(x)
    return out


def emit(g, T, ops):
    eng = {"V": g.vector, "S": g.scalar, "P": g.tensor, "G": g, "Y": g.sync}
    sem = {"V": "sv", "S": "ss", "P": "sp", "G": "sg"}
    cnt = {}
    know = {e: {} for e in eng}
    lastw, readers, snaps = {}, {}, {}

    def wait_for(e, r, w, me):
        need = []
        for k in r:
            if k in lastw:
                need.append((lastw[k], False))
            if k[0] == "p":
                need.extend((x, True) for x in readers.get(k, ()))
        for k in w:
            if k in lastw:
                need.append((lastw[k], True))
            need.extend((x, True) for x in readers.get(k, ()))
        mx = {}
        for (s, c), anti in need:
            if (s == e and (anti or e == "P")) or s == me:
                continue
            if s not in eng:
                c = cnt[s]
            if know[e].get(s, 0) < c:
                mx[s] = max(mx.get(s, 0), c)
        for s in list(mx):
            if any(s2 != s and mx[s2] and snaps.get((s2, mx[s2]), {}).get(s, 0) >= mx[s] for s2 in mx):
                know[e][s] = max(know[e].get(s, 0), mx[s])
                mx[s] = 0
        for s, c in mx.items():
            if c:
                eng[e].wait_ge(T.sem[sem.get(s, s)], c)
                for s2, c2 in snaps.get((s, c), {}).items():
                    know[e][s2] = max(know[e].get(s2, 0), c2)
                know[e][s] = max(know[e].get(s, 0), c)

    for o in ops:
        e, r, w = o["e"], o["r"], o["w"]
        if e == "R":
            cnt[o["sem"]] = 14
            for k in w:
                lastw[k] = (o["sem"], 14)
            continue
        wait_for(e, r, w, o["sem"])
        if o["sem"] == "lsem":
            o["fn"](eng[e])
            continue
        s, add = (o["sem"], 16) if o["sem"] else (e, 1)
        cnt[s] = cnt.get(s, 0) + add
        o["fn"](eng[e]).then_inc(T.sem[sem.get(s, s)], add)
        tok = (s, cnt[s])
        sn = dict(know[e])
        if s in eng:
            sn[s] = cnt[s]
        else:
            for s2, c2 in snaps.get((s, cnt[s] - 16), {}).items():
                sn[s2] = max(sn.get(s2, 0), c2)
        snaps[tok] = sn
        for k in r:
            readers.setdefault(k, []).append(tok)
        for k in w:
            lastw[k] = tok
            readers[k] = []
    for s, c in sorted(cnt.items()):
        if know["G"].get(s, 0) < c:
            g.wait_ge(T.sem[sem.get(s, s)], c)
    g.wait_ge(T.sem.lsem, 28)


def rank_program(g, core, T, topo):
    rank = T.rank_of(core)
    if rank is None:
        return
    ops = []
    ahead = [0.0]

    def op(e, fn, r, w, c, sem=None, lat=0.0, by=0.0):
        ops.append({"e": e, "fn": fn, "r": list(r), "w": list(w), "c": c, "sem": sem, "lat": lat, "by": by,
                    "first": ahead[0] + LOADS.get(sem, 0.0)})

    def V(fn, r, w, n):
        op("V", fn, r, w, FV + max(64, n) * CY)

    def ts(out, in0, s1, s2, op0, op1, r, w, n=64):
        if op1 is None:
            V(lambda v: v.tensor_scalar(out, in0, s1, None, op0), r, w, n)
        else:
            V(lambda v: v.tensor_scalar(out, in0, s1, s2, op0, op1), r, w, n)

    def tt(out, in0, in1, o, r, w, n=64):
        V(lambda v: v.tensor_tensor(out, in0, in1, o), r, w, n)

    def cp(out, in_, r, w, n=64):
        V(lambda v: v.tensor_copy(out, in_), r, w, n)

    def tr(out, in_, r, w, n=64):
        V(lambda v: v.transpose(out, in_), r, w, n)

    def ms(ap, x, w, n=64):
        V(lambda v: v.memset(ap, x), [], w, n)

    def act(out, in_, f, bias, scale, r, w, n):
        op("S", lambda s: s.activation(out, in_, f, bias=bias, scale=scale), r, w, FS + n * CY)

    def mm(out, lhsT, rhs, start, stop, r, w, n):
        op("P", lambda t: t.matmul(out, lhsT, rhs, start, stop), r, w, FP + max(64, n) * PE)

    def dma(e, out, in_, sem, r, w, kb):
        op(e, lambda q: q.dma_start(out=out, in_=in_), r, w, 0.07, sem, 2.0, kb / 200.0)

    B = lambda n, s: T[n + s]
    st = {"A": 0, "B": 1}

    dma("Y", T.W0I[:], T.w0[:], "dw", [], ["W0I"], 12)
    for i in range(8):
        dma("Y", T.ATI[16 * i:16 * i + 15, :], T.lk[16 * i:16 * i + 15, :], "dl", [], ["ATI"], 120)
    dma("Y", T.ATI[15:128:16, :], T.nx[:, :], "dl", [], ["ATI"], 64)
    dma("Y", T.XO[:, 8:2056], T.x0[:, :], "dx", [], ["XOb"], 512)

    def both(sem, src, keys):
        for i in range(8):
            o, a = (i % 2) * H + 8, 32 * (i // 2)
            for par in range(2):
                dma("Y", T.X2[a + 16 * par:a + 16 * par + 16, o:o + 2048], src[16 * i:16 * i + 16, :], sem, keys, ["X2b"], 64)
    both("dy", T.x0, [])

    def iota(out, pat, base, cm, key, n, flag=True):
        if flag:
            op("G", lambda q: q.iota(out, pat, base, cm, allow_small_or_imprecise_dtypes=True), [], [key], 0.13 + 2 * n * CY)
        else:
            op("G", lambda q: q.iota(out, pat, base, cm), [], [key], 0.13 + 2 * n * CY)
    iota(T.PI[:, 0:1], [[1, 1]], 0, 1, "PI", 1, False)
    iota(T.Q[:], [[1, 144]], 0, 0, "Q", 144)
    iota(T.QG[:], [[1, 8], [0, 16]], 0, 0, "QG", 128)
    iota(T.QX2[:], [[0, 8], [1, 16]], 0, 0, "QX2", 128)
    iota(T.QX[:], [[0, 24], [1, 16]], 0, 0, "QX", 384)
    iota(T.DWL[:], [[16, 24]], 2816, 0, "DWL", 24)
    iota(T.QW[:, 0:256], [[32, 8], [0, 2], [1, 16]], 0, 0, "QW", 256, False)
    iota(T.QW[:, 256:512], [[32, 8], [0, 2], [1, 16]], 16, 0, "QW", 256, False)
    iota(T.QW[:, 512:768], [[1, 256]], 0, 0, "QW", 256, False)
    iota(T.NEWL[:], [[1, 384]], 2049, 0, "NEWL", 384)
    iota(T.IDT[:], [[1, 2816]], 0, 0, "IDT", 2816)
    c = lambda i: T.C[:, i:i + 1]
    ms(T.ZR[:], 0.0, ["ZR"])
    for ph in range(2):
        ms(T.X2[:, ph * H:ph * H + 8], 255.0, ["X2n"])
        ms(T.X2[:, ph * H + 2056:ph * H + H], 255.0, ["X2n"], 384)
    ms(T.XO[:, 0:8], 0.0, ["XOn"])
    ms(T.XO[:, 2056:8 + NA], 0.0, ["XOn"], 576)
    ts(T.PI[:, 1:2], T.PI[:, 0:1], 4, None, ALU.arith_shift_right, None, ["PI"], ["PI1"])
    ts(T.PI[:, 2:3], T.PI[:, 0:1], 15, None, ALU.bitwise_and, None, ["PI"], ["PI2"])
    ts(T.PI[:, 3:4], T.PI[:, 0:1], 4, 1, ALU.arith_shift_right, ALU.bitwise_and, ["PI"], ["PI3"])
    ts(T.PI[:, 4:5], T.PI[:, 0:1], 1, None, ALU.bitwise_and, None, ["PI"], ["PI4"])
    cp(T.C[:, 0:5], T.PI[:, 0:5], ["PI", "PI1", "PI2", "PI3", "PI4"], ["C0"])
    for o, i, s1, s2, o0, o1, rr in [
        (6, 2, 15.0, None, ALU.is_equal, None, []),
        (7, 2, 14.0, None, ALU.is_equal, None, []),
        (10, 2, 16.0, -209.0, ALU.mult, ALU.add, []),
        (20, 4, -1.0, 1.0, ALU.mult, ALU.add, []),
        (16, 3, 1000.0, c(0), ALU.mult, ALU.add, []),
        (21, 3, -1000.0, 1000.0, ALU.mult, ALU.add, []),
        (15, 2, -1.0, c(0), ALU.mult, ALU.add, []),
        (8, 6, 1.0e6, 69.5, ALU.mult, ALU.add, [6]),
        (22, 6, -16.0, c(2), ALU.mult, ALU.add, [6]),
        (14, 6, 1.0, None, ALU.subtract, None, [6]),
        (23, 6, -1.0, 1.0, ALU.mult, ALU.add, [6]),
        (12, 20, -2.0, None, ALU.mult, None, [20]),
        (13, 20, 15.0, None, ALU.mult, None, [20]),
        (17, 16, 16.0, None, ALU.add, None, [16]),
        (19, 21, c(0), None, ALU.add, None, [21]),
        (24, 15, 15.0, None, ALU.add, None, [15]),
        (9, 7, -1000.0, c(8), ALU.mult, ALU.add, [7, 8]),
        (11, 22, 2.0, 4096.0, ALU.add, ALU.mult, [22]),
        (18, 19, -16.0, None, ALU.add, None, [19]),
    ]:
        ts(c(o), c(i), s1, s2, o0, o1, ["C0"] + ["C%d" % x for x in rr], ["C%d" % o])
    cp(T.VL0[:], T.W0I[:], ["W0I"], ["VLA", "VLB"])
    for j, col in enumerate((16, 17, 18, 19)):
        ts(T.SWB[:, 128 * j:128 * j + 128], T.Q[:, 0:128], c(col), None, ALU.is_equal, None, ["Q", "C%d" % col], ["SWB"], 128)
    swb = lambda s, d: T.SWB[:, 128 * (2 * s + d):128 * (2 * s + d) + 128]
    swf = lambda s, d: T.SWF[:, 128 * (2 * s + d):128 * (2 * s + d) + 128]
    ts(T.ID[:], T.Q[:, 0:128], c(0), None, ALU.is_equal, None, ["Q", "C0"], ["ID"], 128)
    ts(T.NI[:], T.Q[:, 0:128], c(0), -1.0, ALU.is_equal, ALU.mult, ["Q", "C0"], ["NI"], 128)
    ts(T.ZD[:], T.Q[:], c(24), None, ALU.is_equal, None, ["Q", "C24"], ["ZD"], 144)
    cp(T.SWF[:], T.SWB[:], ["SWB"], ["SWF"], 512)
    ts(T.DW[:], T.Q[:, 0:128], c(0), c(11), ALU.is_equal, ALU.mult, ["Q", "C0", "C11"], ["DW"], 128)
    ts(T.PN[:], T.Q[:, 0:128], c(0), 128.0, ALU.is_equal, ALU.mult, ["Q", "C0"], ["PN"], 128)
    ts(T.BK[:], T.QG[:], c(1), None, ALU.is_equal, None, ["QG", "C0"], ["BK"], 128)
    ts(T.T1[:], T.QX2[:], c(2), -16.0, ALU.is_lt, ALU.mult, ["QX2", "C0"], ["T1"], 128)
    ts(T.T2[:], T.T1[:], 1.0, c(23), ALU.add, ALU.mult, ["T1", "C23"], ["T2"], 128)
    tt(T.TU[:], T.T2[:], T.BK[:], ALU.mult, ["T2", "BK"], ["TU"], 256)
    ts(T.R1[:], T.QX[:], 0.0, None, ALU.is_gt, None, ["QX"], ["R1"], 384)
    ms(T.AT[:, 2048:NA], -1.0, ["ATn"], 1152)
    ts(T.DIAG[:], T.QX[:], c(2), None, ALU.is_equal, None, ["QX", "C0"], ["DIAG"], 384)
    ts(T.TRI[:], T.QX[:], c(2), None, ALU.is_gt, None, ["QX", "C0"], ["TRI"], 384)
    ts(T.NEWL[:], T.NEWL[:], c(7), None, ALU.mult, None, ["NEWL", "C7"], ["NEWL"], 384)
    ts(T.DWL[:], T.DWL[:], c(2), None, ALU.add, None, ["DWL", "C0"], ["DWL"])
    ts(T.QW[:], T.QW[:], 127, None, ALU.bitwise_and, None, ["QW"], ["QW"], 768)
    ts(T.W3[:], T.QW[:], c(0), None, ALU.is_equal, None, ["QW", "C0"], ["W3"], 768)

    sl = lambda s: slice(12 * st[s], 12 * st[s] + 12)
    sw = lambda s: slice(192 * st[s], 192 * st[s] + 192)
    X2ALL, XOALL = ["X2b", "X2n"], ["XOb", "XOn"]

    def vx_lists(s, src, key):
        for u in range(2):
            o = 12 * st[s] + 6 * u
            ts(T.VX0[:, o:o + 6], src(u), 8.0, None, ALU.add, None, [key], ["VX" + s])

    for s in "AB":
        vx_lists(s, lambda u: T.W0I[:, 12 * st[s] + u:12 * st[s] + 12:2], "W0I")
    cp(T.AT[:, 0:2048], T.ATI[:], ["ATI"], ["AT"], 2048)

    def agather(s, key=True):
        act(T.GA[:, sw(s)], T.AT[:].indirect(T.VL0[:, sl(s)]), ACT.Identity, 0.0, 1.0, ["AT", "ATn", "VL" + s], ["GA" + s], 192 * GA_C)
        if key:
            dma("Y", T.GA3[:, sl(s), :], T.GA[:, sw(s)], "dg" + s, ["GA" + s], ["G3" + s], 96)

    def xgather(s):
        act(T.XV[:, sw(s)], T.XO[:].indirect(T.VX0[:, sl(s)]), ACT.Identity, 0.0, 1.0, XOALL + ["VX" + s], ["XV" + s], 192 * GA_C)

    def swap4(out, o0, mat, src, key, r, stop, n=1, f=1):
        k = 0
        for rep in range(n):
            for u in range(2):
                for v in range(2):
                    k += 1
                    mm(out[:, o0 + v:o0 + 12:2, :], mat(v, u), src(u), False, stop and k == 4 * n, r, [key], 96 * f)

    def xv(s):
        return lambda u: T.XV[:, 192 * st[s] + 96 * u:192 * st[s] + 96 * u + 96]

    def zswap(s, first):
        o = B("pZ", s)
        if first:
            mm(o[:, 0:12, :], T.ZR[:], T.XV[:, sw(s)], True, False, ["ZR", "XV" + s], ["pZ" + s], 192)
        else:
            mm(o[:, 0:12, :], T.ID[:], B("Z", s)[:, 0:192], True, False, ["ID", "Z" + s], ["pZ" + s], 192)
        swap4(o, 0, swb, xv(s), "pZ" + s, ["XV" + s, "SWB"], True, 2 if first else 1)

    def zact(s, first, final=False):
        bias = 127.75 if first else 63.75
        src = B("pZ", s)[:, 0:12, :]
        if final:
            act(B("ZF", s)[:], src, ACT.Identity, bias, 0.5, ["pZ" + s], ["ZF" + s], 192)
        else:
            for d in range(2):
                act(B("Z", s)[:, 192 * d:192 * d + 192], src, ACT.Identity, bias, 0.5, ["pZ" + s], ["Z" + s], 192)

    def lists(s, L):
        lt, cl = B("LT", s), B("CL", s)
        for b in range(6):
            o = 192 * st[s] + 32 * b
            tr(lt[:, b:192:6], T.GA[:, o:o + 32], ["GA" + s], ["LT" + s])
        for g2 in range(2):
            ts(cl[:, g2:12 * L:2], lt[:, 96 * g2:96 * g2 + 6 * L], 8.0 + H * g2, None, ALU.add, None, ["LT" + s], ["CL" + s], 90)

    def begin(s, L):
        agather(s)
        xgather(s)
        zswap(s, True)
        zact(s, True)
        lists(s, L)

    def bulk(s, k, t):
        L = 14 + t
        pd, ab, cd, cl, z = B("pD", s), B("AB", s), B("CD", s), B("CL", s), B("Z", s)
        for i in range(0, 2 * NB, 2):
            act(B("XG", s)[:], T.X2[:].indirect(cl[:, 12 * i:12 * i + 24]), ACT.Identity, 0.0, 1.0, X2ALL + ["CL" + s], ["XG" + s], 384 * GA_C)
            o = B("pS", s)[:, 0:24, :]
            mm(o, T.ID[:], B("XG", s)[:], True, False, ["ID", "XG" + s], ["pS" + s], 384)
            mm(o, T.NI[:], z[:], False, True, ["NI", "Z" + s], ["pS" + s], 384)
            act(ab[:, 192 * i:192 * i + 384], o, ACT.Abs, 128.0, 1.0, ["pS" + s], ["AB%s%d" % (s, i), "AB%s%d" % (s, i + 1)], 384)
        for i in range(2 * NB, L, 2):
            n = min(2, L - i)
            tt(cd[:, 192 * i:192 * (i + n)], T.X2[:].indirect(cl[:, 12 * i:12 * (i + n)]), z[:, 0:192 * n], ALU.subtract,
               X2ALL + ["CL" + s, "Z" + s], ["CD%s%d" % (s, x) for x in range(i, i + n)], 192 * n * GA_C)
        for i, n in ABS:
            n = min(n, L - i)
            act(ab[:, 192 * i:192 * (i + n)], cd[:, 192 * i:192 * (i + n)], ACT.Abs, 128.0, 1.0,
                ["CD%s%d" % (s, x) for x in range(i, i + n)], ["AB%s%d" % (s, x) for x in range(i, i + n)], 192 * n)
        if k:
            mm(pd[:, 0:192], T.PN[:], B("F", s)[:], True, False, ["PN", "F" + s], ["pD" + s], 192)
        todo = [x for i in ORDER for x in (i, i + 1)] + [14] * t
        for j, x in enumerate(todo):
            mm(pd[:, 0:192], T.ZD[:, 15 - x:143 - x], ab[:, 192 * x:192 * x + 192], j == 0 and not k, j == L - 1,
               ["ZD", "AB%s%d" % (s, x)], ["pD" + s], 192)
        o = B("pK", s)
        mm(o[:, 0:12, :], T.ZR[:], z[:, 0:192], True, False, ["ZR", "Z" + s], ["pK" + s], 192)
        swap4(o, 0, swf, lambda u: T.GA3[:, 12 * st[s] + u:12 * st[s] + 12:2, :], "pK" + s, ["G3" + s, "SWF"], False, 1, 4)

    def select(s, k, t):
        L = 14 + t
        last = k == 3
        thr = 8 if t else 9
        kt, sc, vi, vj = B("KT", s), B("SC", s), B("VI", s), B("VJ", s)
        act(B("VAL", s)[:], B("pD", s)[:, 0:192], ACT.Sign, c(thr), -1.0, ["pD" + s, "C%d" % thr], ["VAL" + s], 192)
        mm(B("pK", s)[:, 0:12, :], T.DW[:], B("VAL", s)[:], False, True, ["DW", "VAL" + s], ["pK" + s], 192)
        tr(kt[:], B("pK", s)[:, 0:12, :], ["pK" + s], ["KT" + s], 192)
        V(lambda v: v.tensor_tensor_scan(sc[:], T.R1[:, 0:192], kt[:], 0.0, ALU.mult, ALU.max), ["R1", "KT" + s], ["SC" + s], 192)
        cp(vi[:], sc[:, 15:192:16], ["SC" + s], ["VI" + s])
        ts(vj[:], vi[:], 4095, None, ALU.bitwise_and, None, ["VI" + s], ["VJ" + s])
        cp(T.VL0[:, sl(s)], vj[:], ["VJ" + s], ["VL" + s])
        vx_lists(s, lambda u: vj[:, u:12:2], "VJ" + s)
        if last:
            cp(T.VLF[:, sl(s)], vj[:], ["VJ" + s], ["VLF" + s])
            ts(T.VXN[:, sl(s)], vj[:], 8.0, None, ALU.add, None, ["VJ" + s], ["VXN" + s])
        else:
            o = B("pD", s)[:, 192:384]
            mm(o, T.TU[:], B("VAL", s)[:], True, k == 0, ["TU", "VAL" + s], ["pD" + s], 192)
            if k:
                mm(o, T.ID[:], B("F", s)[:], False, True, ["ID", "F" + s], ["pD" + s], 192)
            act(B("F", s)[:], o, ACT.Relu, c(10), 1.0, ["pD" + s, "C10"], ["F" + s], 192)
        if not (last and t):
            agather(s, not last)
        xgather(s)
        zswap(s, False)
        if last:
            o = B("pS", s)
            mm(o[:, 0:12, :], T.NI[:], B("Z", s)[:, 0:192], True, False, ["NI", "Z" + s], ["pS" + s], 192)
            swap4(o, 0, swb, xv(s), "pS" + s, ["XV" + s, "SWB"], True)
        zact(s, False, last)
        if not last:
            lists(s, L)

    def votes(s, t):
        act(B("GT", s)[:], B("pS", s)[:, 0:12, :], ACT.Sign, 127.5, 1.0, ["pS" + s], ["GT" + s], 192)
        mm(B("pK", s)[:, 0:12, :], T.BK[:], B("GT", s)[:], True, True, ["BK", "GT" + s], ["pK" + s], 192)
        o = B("pZ", s)
        mm(o[:, 12:24, :], T.ZR[:], B("ZF", s)[:], True, False, ["ZR", "ZF" + s], ["pZ" + s], 192)
        swap4(o, 12, swb, lambda u: B("ZF", s)[:, u:12:2, :], "pZ" + s, ["ZF" + s, "SWB"], True)
        zn = "ZN%d" % t
        act(T[zn][:, sw(s)], o[:, 12:24, :], ACT.Identity, 0.0, 1.0, ["pZ" + s], [zn + s], 192)
        act(T.VF[:, sw(s)], T.IDT[:].indirect(T.VL0[:, sl(s)]), ACT.Identity, 0.0, 1.0, ["IDT", "VL" + s], ["VF" + s], 192 * GA_C)
        tr(B("KT", s)[:], B("pK", s)[:, 0:12, :], ["pK" + s], ["KT" + s], 192)
        ts(T.WT[:, sl(s)], B("KT", s)[:, 0:192:16], 1.0, EPS, ALU.is_lt, ALU.add, ["KT" + s], ["WT" + s])
        for d in range(2):
            cp(T.VB[:, 24 * d + 12 * st[s]:24 * d + 12 * st[s] + 12, :], T.VF[:, sw(s)], ["VF" + s], ["VB" + s], 192)
        if s == "A":
            cp(T.VB[:, 48:49, :], T.VF[:, 0:16], ["VFA"], ["VBA"])
        trs = []
        for q in range(4 * st[s], 4 * st[s] + 4):
            if q == rank:
                continue
            dst = T.cores[q]
            rid, pid, _e = topo.addr(dst)
            j = 2 * len(trs)
            mask = sum(1 << e for e in topo.engines(core, dst)[j:j + 2])
            trs.append(RemoteDMATransfer(dst_ids=[DstId(rid=rid, pnc=pid)], dma_engine_mask=mask, remote_sem=T.sem["arr%d" % t],
                                         src=T[zn][:, 48 * q:48 * q + 48], dst=T["RZ%d" % t][:, 48 * rank:48 * rank + 48]))
        op("G", lambda q: q.remote_dma_fused(trs, local_sem=T.sem.lsem), [zn + s], [], 1.0, "lsem")

    def flips(t):
        rest, ear, gas, zn = T.pKA, T.pKB, ["GAA", "GAB"], "ZN%d" % t
        act(T.XW[:], T.XO[:].indirect(T.VXN[:]), ACT.Identity, 0.0, 1.0, XOALL + ["VXNA", "VXNB"], ["XW"], 384 * GA_C)
        act(T.DX[:], T.XW[:], ACT.Identity, c(13), c(12), ["XW", "C12", "C13"], ["DX"], 384)
        mm(ear[:, 0:24, :], T.ZR[:], T[zn][:], True, False, ["ZR", zn + "A", zn + "B"], ["pKB"], 384)
        for b in range(23, -1, -1):
            e0 = 24 * b
            ts(T.E[:, e0:e0 + 24, :], T.VB[:, b + 1:b + 25, :], T.VLF[:, b:b + 1], T.WT[:, b:b + 1], ALU.is_equal, ALU.mult,
               ["VBA", "VBB", "VLFA", "VLFB", "WTA", "WTB"], ["E%d" % b], 192)
            if b < 23:
                mm(ear[:, b + 1:24, :], T.BK[:], T.E[:, e0:e0 + 23 - b, :], False, False, ["BK", "E%d" % b], ["pKB"], 368 - 16 * b)
            mm(rest[:, 0:b + 1, :], T.BK[:], T.E[:, e0 + 23 - b:e0 + 24, :], b == 23, b == 0, ["BK", "E%d" % b], ["pKA"], 16 + 16 * b)
        for h in (18, 12, 6, 0):
            tt(T.DG[:, h:h + 6, :], T.E[:, 24 * h + 23:24 * h + 144:24, :], T.TRI[:, h:h + 6, :], ALU.mult,
               ["E%d" % b for b in range(h, h + 6)] + ["TRI"], ["DG"], 192)
        act(T.RS[:], rest[:, 0:24, :], ACT.Identity, 0.0, 1.0, ["pKA"], ["RS"], 384)
        mm(ear[:, 0:24, :], T.BK[:], T.DG[:], False, True, ["BK", "DG"], ["pKB"], 384)
        tt(T.S3[:], T.DWL[:], T.VLF[:], ALU.subtract, ["DWL", "VLFA", "VLFB"], ["S3"])
        tt(T.DM[:], ear[:, 0:24, :], T.DIAG[:], ALU.mult, ["pKB", "DIAG"], ["DM"], 384)
        tt(T.RT[:], ear[:, 0:24, :], T.RS[:], ALU.add, ["pKB", "RS"], ["RT"], 384)
        V(lambda v: v.tensor_tensor_scan(T.SC2[:], T.R1[:], T.DM[:], 0.0, ALU.mult, ALU.add), ["R1", "DM"], ["SC2"], 384)
        ts(T.pZA[:, 0:24, :], T.RT[:], 1.0, None, ALU.is_lt, None, ["RT"], ["pZA"], 384)
        ts(T.S1[:], T.SC2[:, 15:384:16], 0.0, None, ALU.is_gt, None, ["SC2"], ["S1"])
        tt(T.S2[:], T.S1[:], T.S3[:], ALU.mult, ["S1", "S3"], ["S2"])
        tt(T.FX[:], T.pZA[:, 0:24, :], T.DX[:], ALU.mult, ["pZA", "DX"], ["FX"], 384)
        tt(T.S4[:], T.S2[:], T.VLF[:], ALU.add, ["S2", "VLFA", "VLFB"], ["S4"])
        ts(T.XOFF[:], T.S4[:], 8.0, None, ALU.add, None, ["S4"], ["XOFF"])
        tt(T.XO[:].indirect(T.XOFF[:]), T.XW[:], T.FX[:], ALU.add, ["XW", "FX", "XOFF"], XOALL, 384 * SC_C)
        if not t:
            both("dd", T.XO[:, 8:2056], ["XOb"])
            cp(T.AOFF[:], T.S4[:], ["S4"], ["AOFF"])
            act(T.AT[:, 2048:2432], T.GA[:], ACT.Identity, c(14), c(6), gas + ["C6", "C14"], ["ATn"], 384)
            tt(T.AT[:].indirect(T.AOFF[:]), T.GA[:], T.NEWL[:], ALU.add, gas + ["NEWL", "AOFF"], ["AT", "ATn"], 384 * SC_C)

    def arrivals(t):
        rz, zn = "RZ%d" % t, "ZN%d" % t
        op("R", None, [zn + "A", zn + "B"], [rz], 8.0, "arr%d" % t)
        for ph, pk in ((0, "pSA"), (1, "pSB"), (2, "pZB"))[2 * t:]:
            for r in range(8):
                d = (rank - r) % 8
                if ph == 2:
                    o = 512 + 128 - 16 * d
                else:
                    e = (ph - d) % 2
                    o = 256 * e + 32 * ((((ph - d) % 8 - e) // 2) % 4)
                src, keys = (T[zn], [zn + "A", zn + "B"]) if r == rank else (T[rz], [rz])
                mm(T[pk][:, 3 * r:3 * r + 3, :], T.W3[:, o:o + 128], src[:, 48 * r:48 * r + 48], True, True, ["W3"] + keys, [pk], 64)
            n = 8 + 2048
            if t:
                out, key = T.XM[:], "XM"
            elif ph == 2:
                out, key = T.XO[:, n:n + 384], "XOn"
            else:
                out, key = T.X2[:, ph * H + n:ph * H + n + 384], "X2n"
            act(out, T[pk][:, 0:24, :], ACT.Identity, -128.0, 1.0, [pk], [key], 384)

    for t in range(2):
        for s in "AB":
            begin(s, 14 + t)
        for k in range(4):
            for s in "AB":
                ahead[0] = AHEAD if s == "A" else 0.0
                bulk(s, k, t)
                select(s, k, t)
        ahead[0] = 0.0
        for s in "AB":
            votes(s, t)
        if t:
            dma("Y", T.yv[:, :], T.VF[0:128:16, :], "dv", ["VFA", "VFB"], [], 12)
            arrivals(t)
        flips(t)
        if not t:
            arrivals(t)
    dma("Y", T.yx[:, 2432:2816], T.XM[:], "dv", ["XM"], [], 96)
    dma("Y", T.yx[:, 0:2432], T.XO[:, 8:2440], "do", XOALL, [], 620)
    emit(g, T, schedule(ops))
